import numpy as np, ml_dtypes
CORES = [1,5,17,21,33,37,49,53]
N = 8
import mx_ref
BF = ml_dtypes.bfloat16
def entries(a):
    return np.ascontiguousarray(a.T).reshape(-1)
def table(e):
    return np.ascontiguousarray(np.reshape(e, (-1, 16)).T).astype(np.int32)
def gcols(t, e):
    v = np.concatenate([t.reshape(8, 16, -1, 4), np.zeros((8, 16, 1, 4), BF)], axis=2)
    return np.ascontiguousarray(np.stack([v[g][:, e[g]] for g in range(8)])).reshape(128, -1)
def tile(rs):
    return np.stack(rs, axis=2).reshape(128, -1).astype(BF)
def pick(q, e):
    c = np.concatenate([q[0].reshape(128, -1, 4), np.zeros((128, 1, 4), np.uint8)], axis=1); s = np.concatenate([q[1], np.ones((16, 1), np.uint8)], axis=1)
    return (np.ascontiguousarray(c[:, e].reshape(128, -1)), np.ascontiguousarray(s[:, e]))
def join(*qs):
    return (np.concatenate([q[0] for q in qs], axis=1), np.concatenate([q[1] for q in qs], axis=1))
def put(q, e, v):
    c, s = q[0].reshape(128, -1, 4).copy(), q[1].copy(); c[:, e] = v[0].reshape(128, -1, 4); s[:, e] = v[1]
    return (c.reshape(128, -1), s)
def pk(c, s):
    return (np.ascontiguousarray(c), mx_ref.live(s))
def emit(q):
    return q[0], q[1]
def packed(v, rng):
    q = [mx_ref.quantize(np.ascontiguousarray(v[r])) for r in range(N)]
    return np.stack([a for a, b in q]), np.stack([mx_ref.plane(b, rng) for a, b in q])
def values_of_codes():
    e, c = np.zeros((128, 128, 4), np.float32), np.zeros((128, 2, 4), np.uint8)
    e[np.arange(128), np.arange(128), 0] = 1
    c[:127, :, 0] = np.arange(256).reshape(2, 128).T[:127]
    return mx_ref.matmul(mx_ref.quantize(e.reshape(128, 512).astype(BF)), (c.reshape(128, 8), np.full((16, 2), 127, np.uint8))).T.reshape(-1).astype(np.float64)
CODE_VALUE, SCALE_VALUE = values_of_codes(), 2.0 ** (np.arange(256) - 127.0)
def decode(q):
    return (CODE_VALUE[q[0]].reshape(16, 8, -1, 4) * SCALE_VALUE[q[1]][:, None, :, None] + 0.0).reshape(128, -1).astype(np.float32)
def f(rng, *shape):
    return mx_ref.flush((rng.standard_normal(shape, dtype=np.float32) * np.exp2(rng.integers(-2, 3, shape[:-1] + (1,)))).astype(BF))
def wide(rng, *shape, cols=0):
    v = rng.standard_normal(shape, dtype=np.float32) * np.exp2(rng.integers(-12, 13, shape)).astype(np.float32)
    if cols: v *= np.repeat(np.exp2(rng.integers(-cols, cols + 1, shape[:-2] + (1, shape[-1] // 4))) * (rng.random(shape[:-2] + (1, shape[-1] // 4)) > 0.0625), 4, axis=-1).astype(np.float32)
    return mx_ref.flush(v.astype(BF))
C, TH, R = 320, 240, 3
def big(v):
    v = v.astype(np.float32)
    v[np.abs(v) < np.float32(2.0 ** -16)] = 0
    return v.astype(BF)
def numbers_of(rng):
    return {"x": big(f(rng, N, 128, 4 * C)), "u": np.array(f(rng, N, 128, 512)), "v": np.array(f(rng, N, 128, 512))}
def offers(rng):
    return np.stack([table(rng.integers(0, C, 8 * R * C)) for r in range(N)])
def layers(rng):
    return big(f(rng, N, 128, 2048)).reshape(N, 8, 16, 4, 8, 16, 4)
def weights(rng, w):
    c, p = packed(np.ascontiguousarray(w).reshape(N, 128, 2048), rng)
    return {"wc": c, "ws": p}
def setup_inputs(rng):
    return {**numbers_of(rng), "cd": offers(rng), **weights(rng, layers(rng))}
def setup_inputs_ties(rng):
    d = numbers_of(rng)
    x = d["x"].astype(np.float32).reshape(N, 8, 16, C, 4)
    x[:, :, 0] = 0
    k = rng.integers(-2, 3, (N, 4, C))
    for r in range(N): x[r, :, 0, :, 0] = k[r][rng.permutation(8) % 4]
    u = d["u"].reshape(N, 128, 128, 4)
    u[:, :, ::16] = 0
    o = rng.permutation(N)
    for r in range(N):
        for h in range(0, 128, 16): u[r, h, h, 0] = 0.0 if r == o[0] else -1.0 if r == o[1] else 1.0
    w = layers(rng)
    w[:, :, :, :, :, 0] = 0
    return {"x": x.reshape(N, 128, 4 * C).astype(BF), "u": u.reshape(N, 128, 512), "v": d["v"], "cd": offers(rng), **weights(rng, w)}
def setup_inputs_near(rng):
    d = numbers_of(rng)
    x = d["x"].astype(np.float32).reshape(N, 8, 16, C, 4)
    x[:, :, 0] = 0
    x[:, :, 8:] = 0
    u = d["u"].reshape(N, 128, 128, 4)
    u[:, :, ::16] = 0
    o = rng.permutation(N) % 4
    for r in range(N):
        s = rng.integers(0, 256, (8, C))
        if o[r] < 3:
            for b in range(8): x[r, :, 8 + b // 4, :, b % 4] = ((s >> b) & 1) * 2.0 ** (b - 23)
        else: x[r, :, 10, :, 0] = (8 + s % 8) * 2.0 ** -33
        if o[r] < 2:
            x[r, :, 0, :, 0] = rng.permutation(8)[:, None] % 2 * 2.0 - 1.0
            x[r, :, 11, :, 0] = 2.0 ** -10
        for g in rng.permutation(8)[:4]:
            j = rng.integers(C)
            x[r, g, 8:, j] = 0
            x[r, g, 8 if o[r] < 3 else 10, j, 0] = rng.choice([-1.0, 1.0]) * 2.0 ** 30
        for h in range(0, 128, 16):
            k = 1.0 if o[r] == 0 else 2.0 ** -30
            if o[r] > 1: k = k * rng.choice([-1.0, 1.0])
            if o[r] < 2:
                u[r, h, h, 0] = k
                u[r, h + 11, h, 0] = k
            if o[r] < 3: u[r, h + 8:h + 10, h] = k
            else: u[r, h + 10, h, 0] = k
    w = layers(rng)
    w[:, :, 0] = 0
    w[:, :, 8:] = 0
    w[:, :, :, :, :, 0] = 0
    w[:, :, :, :, :, 8:] = 0
    return {"x": x.reshape(N, 128, 4 * C).astype(BF), "u": u.reshape(N, 128, 512), "v": d["v"], "cd": offers(rng), **weights(rng, w)}
def setup_inputs_huge(rng):
    d = numbers_of(rng)
    o = rng.permutation(N)
    c = rng.choice([-1.0, 1.0], (N, 1, 1, C, 1))
    c[o < N // 2] = c[o < N // 2][:, :, :, :1]
    x = (0.6 + 0.09 * rng.random((N, 8, 16, C, 4))) * 2.0 ** 30 * c
    u = d["u"].reshape(N, 128, 128, 4)
    for r in range(N):
        a = np.full((128, 8, 4), 2.0 ** 30)
        if 0 < o[r] < N - 1: a = 2.0 ** 29 * (1.0 - 0.1 * rng.random((128, 8, 4)))
        if o[r] < N // 2: a = a * (rng.permutation(8) % 2 * 2.0 - 1.0)[None, :, None]
        u[r, :, ::16] = a.astype(np.float32).astype(BF)
    w = np.zeros((N, 128, 4, 128, 4), np.float32)
    i = np.arange(128)
    for b in range(4): w[:, i, b, i, b] = 4
    return {"x": x.astype(np.float32).reshape(N, 128, 4 * C).astype(BF), "u": u.reshape(N, 128, 512), "v": d["v"], "cd": offers(rng), **weights(rng, w.astype(BF))}
def setup_inputs_few(rng):
    d = numbers_of(rng)
    x = np.zeros((N, 8, 16, C, 4), np.float32)
    x[:, :, 1, :, 0] = 1.96875
    x[:, :, 2:4] = (129 + 2 * rng.integers(0, 64, (N, 8, 2, C, 4))) * np.exp2(-7.0 - rng.integers(8, 15, (N, 8, 2, C, 4))) * rng.choice([-1.0, 1.0], (N, 8, 2, C, 4))
    u = d["u"].reshape(N, 128, 128, 4)
    u[:, :, ::16] = 0
    for h in range(0, 128, 16): u[:, h, h, 0] = 1
    o, lists = rng.permutation(N), []
    for r in range(N):
        p = rng.permutation(C)
        s = rng.integers(8, 16, (8, C)) * 0.125
        s[:, p[TH:]] *= -1.0
        x[r, :, 0, :, 0] = s
        k = (rng.permutation(R * C) % 4).reshape(R, 1, C)
        low, high, e = p[rng.integers(TH, C, (R, 8, C))], p[rng.integers(0, TH, (R, 8, C))], rng.integers(0, C, (R, 8, C))
        e = np.where(k == 0, low, np.where(k == 1, high, np.where(k == 2, e, e[:, :1])))
        if r == o[0]: e = np.zeros((R, 8, C), np.int64)
        if r == o[1]: e = np.full((R, 8, C), C - 1)
        lists.append(table(e))
    w = np.zeros((N, 8, 16, 4, 8, 16, 4), np.float32)
    w[:, :, 2:4, :, :, 8:] = rng.choice([-1.0, 1.0], (N, 8, 2, 4, 8, 8, 4))
    return {"x": x.reshape(N, 128, 4 * C).astype(BF), "u": u.reshape(N, 128, 512), "v": d["v"], "cd": np.stack(lists), **weights(rng, w.astype(BF))}
def setup_inputs_spread(rng):
    d = setup_inputs(rng)
    d["x"] = big(wide(rng, N, 128, 4 * C, cols=6))
    return d
def check_inputs(d):
    b = []
    for k in ("x", "u", "v"):
        a = np.abs(d[k].astype(np.float32))
        if not (np.isfinite(a).all() and ((a == 0) | (a >= 2.0 ** -30) & (a <= 2.0 ** 30)).all()): b.append("a value of " + k)
    if not ((d["cd"] >= 0) & (d["cd"] < C)).all(): b.append("an entry of cd")
    none, least, most = [emit(mx_ref.quantize(np.full((128, 16), k, np.float32).astype(BF)))[1][0, 0] for k in (0.0, 2.0 ** -30, 2.0 ** 30)]
    for r in range(N):
        if ((d["wc"][r] == 0x7F) | (d["wc"][r] == 0xFF)).any(): b.append("wc: a code that is no number")
        s = mx_ref.live(d["ws"][r])
        if ((s != none) & ((s < least) | (s > most))).any(): b.append("ws: a scale out of range")
    return b
def reference(x, u, v, cd, wc, ws):
    qu = [mx_ref.quantize(u[r]) for r in range(N)]
    lay = [pk(wc[r], ws[r]) for r in range(N)]
    give = [entries(cd[r]).reshape(R, 8, C) for r in range(N)]
    now = [x[r] for r in range(N)]
    lead, i = np.zeros((N, 8, C), np.int64), np.arange(C)
    for t in range(R):
        q = [mx_ref.quantize(now[r]) for r in range(N)]
        own = [decode(q[r]) for r in range(N)]
        place = np.zeros((N, 8, C), np.int64)
        for r in range(N):
            s = mx_ref.matmul(qu[r], q[r])[::16] + np.float32(0.0)
            np.put_along_axis(place[r], np.argsort(-s, axis=1, kind="stable"), i[None, :], axis=1)
        made = [None] * N
        for d in range(N):
            r = (d - 1 - t) % N
            c = give[d][t]
            p = place[d][:, c]
            visit = np.argsort(place[r], axis=0, kind="stable")
            left = np.ones((8, C), bool)
            for g in visit:
                a = p[g, :, i].T
                stay = left & (a < TH)
                left = np.where(np.any(stay, axis=0), stay, left)
                k = np.argmin(np.where(left, a, C), axis=0)
                lead[d, g, i] = c[k, i]
            z = mx_ref.quantize(gcols(own[d].astype(BF), lead[d]))
            h = tile([np.maximum(mx_ref.matmul(pick(lay[d], np.arange(128 * b, 128 * b + 128)), z), np.float32(0.0)) * np.float32(0.015625) for b in range(4)])
            made[r] = (own[r] + decode(mx_ref.quantize(h))).astype(BF)
        now = made
    y, el = np.zeros((N, 128, C), np.float32), np.zeros((N, 8, C), np.float32)
    oc, osc = np.zeros((N, 128, 4 * C), np.uint8), np.zeros((N, 16, C), np.uint8)
    for r in range(N):
        q = mx_ref.quantize(now[r])
        y[r] = mx_ref.matmul(mx_ref.quantize(v[r]), q)
        el[r] = lead[r]
        oc[r], osc[r] = emit(q)
    return {"y": y, "el": el, "oc": oc, "osc": osc}

@@ -1,0 +1,521 @@
+import math
+from concourse.mybir import dt, AluOpType, ActivationFunctionType
+
+C, TH, R, N = 320, 240, 3, 8
+H = C // 2
+NA = (10, 9)
+F32, BF, I32, U16, Q4, U8 = "float32", "bfloat16", "int32", "uint16", "float8_e4m3fn_x4", "uint8"
+
+
+def _s(n, d):
+    return ("sbuf", [128, n], d)
+
+
+SCRATCH = {
+    "xt": _s(4 * C, BF), "ut": _s(512, BF), "vt": _s(512, BF), "cdl": _s(448, I32),
+    "uq": _s(128, Q4), "us": _s(128, U8), "urq": _s(128, Q4), "urs": _s(128, U8), "vq": _s(128, Q4), "vs": _s(128, U8),
+    "wq": _s(512, Q4), "wsc": _s(512, U8),
+    "ones": _s(128, BF), "ident": _s(128, BF), "et": _s(2048, BF), "eq": _s(512, Q4), "es": _s(512, U8),
+    "cmi": _s(512, BF), "ct": _s(1024, BF), "cq": _s(256, Q4), "cs": _s(256, U8),
+    "ip": _s(2, I32), "bi": _s(8, I32), "bf": _s(8, F32), "cf": _s(4, F32), "fi": _s(192, F32), "fo": _s(192, F32),
+    "li": _s(112, I32), "lu": _s(112, U16), "cdu": _s(120, U16),
+    "i16": _s(C, F32), "ij": _s(C, F32), "ijg": _s(C, F32), "ic": _s(C, F32), "negm": _s(C, F32), "rst": _s(C, F32),
+    "keep": _s(C, BF), "rmin": _s(160, F32), "warm": _s(2, F32),
+    "pm": _s(C, F32), "th": _s(C, F32), "sg": _s(sum(NA) * H, BF),
+    "gk": _s(160, F32), "tk": _s(C, F32), "fl": _s(C, BF), "ps": _s(C, BF),
+    "pcw": _s(C, F32), "gc1": _s(640, F32), "tg": _s(640, F32), "bad": _s(C, BF), "sb": _s(C, F32), "pc2": _s(160, I32),
+    "ub": _s(160, F32), "dd": _s(C, BF), "vv": _s(C, BF), "yy": _s(480, F32),
+    "mn": _s(160, F32), "e1": _s(40, I32), "eo": _s(20, U16), "elb": _s(C, F32),
+    "dtw": _s(4 * C, BF), "zt": _s(4 * C, BF), "ht": _s(4 * C, BF), "xn": _s(4 * C, BF), "yb": _s(C, F32),
+}
+for _i in range(7):
+    SCRATCH["ft%d" % _i] = _s(4 * C, BF)
+    SCRATCH["fq%d" % _i] = _s(C, Q4)
+    SCRATCH["fs%d" % _i] = _s(C, U8)
+for _i in range(R + 1):
+    SCRATCH["tq%d" % _i] = _s(C, Q4)
+    SCRATCH["ts%d" % _i] = _s(C, U8)
+for _i in range(R):
+    for _n in ("z", "h", "l"):
+        SCRATCH["%sq%d" % (_n, _i)] = _s(C, Q4)
+        SCRATCH["%ss%d" % (_n, _i)] = _s(C, U8)
+    SCRATCH["wo%d" % _i] = _s(80, BF)
+    SCRATCH["wl%d" % _i] = _s(80, BF)
+for _i in range(8):
+    SCRATCH["pb%d" % _i] = ("psum", [128, 512], F32)
+
+SEMAPHORES = (["cV", "cA", "cP", "cG", "left"] + ["wa%d" % i for i in range(R)] + ["ha%d" % i for i in range(2 * R)]
+              + ["d%d" % i for i in range(12)])
+
+LISTS = {"u": (0, 8), "own": (8, 10), "cmp": (18, 20), "bad": (38, 20), "sel": (58, 10), "w": (68, 20), "v": (88, 10),
+         "uu": (98, 10)}
+SV, SA, CNT, DTB = (0, 2), (1, 7), 5, (3, 4, 6, 0)
+
+
+def rank_program(g, core, T, topo):
+    rank = T.rank_of(core)
+    if rank is None:
+        return
+    A = AluOpType
+    AF = ActivationFunctionType
+    Q = {"V": g.vector, "A": g.scalar, "P": g.tensor, "G": g, "S": g.sync}
+    count = {}
+    known = {q: {} for q in Q}
+    clocks = {}
+    writer, readers = {}, {}
+
+    def wait(q, tok):
+        sem, n = tok
+        k = known[q]
+        if k.get(sem, 0) >= n:
+            return
+        Q[q].wait_ge(T.sem[sem], n)
+        k[sem] = n
+        for s2, n2 in clocks.get(tok, {}).items():
+            if k.get(s2, 0) < n2:
+                k[s2] = n2
+
+    def op(q, fn, r=(), w=(), sem=None, inc=1, x=()):
+        deps = []
+        for key in tuple(r) + tuple(x):
+            if key in writer:
+                deps.append(writer[key])
+        for key in x:
+            deps.extend(t for t in readers.get(key, ()) if t[0] != "c" + q)
+        for key in w:
+            if key in writer and not (q == "P" and writer[key][0] == "cP"):
+                deps.append(writer[key])
+            deps.extend(readers.get(key, ()))
+        deps.sort(key=lambda t: -t[1])
+        for t in deps:
+            wait(q, t)
+        sem = sem or "c" + q
+        count[sem] = count.get(sem, 0) + inc
+        tok = (sem, count[sem])
+        fn().then_inc(T.sem[sem], inc)
+        clocks[tok] = dict(known[q])
+        for key in w:
+            writer[key] = tok
+            readers[key] = []
+        for key in tuple(r) + tuple(x):
+            readers.setdefault(key, []).append(tok)
+        return tok
+
+    def arrives(key, sem, n):
+        count[sem] = n
+        writer[key] = (sem, n)
+        readers[key] = []
+
+    V, S_, P = g.vector, g.scalar, g.tensor
+
+    def lst(name, a=0, b=None):
+        c0, n = LISTS[name]
+        return T.lu[:, c0 + a:c0 + (n if b is None else b)]
+
+    def quant(qb, sb, tb, a, b, r, w):
+        return op("V", lambda: V.quantize_mx(qb[:, a:b], sb[:, a:b], tb[:, 4 * a:4 * b]), r=r, w=w)
+
+    def mm(bank, lq, ls, k, rq, rs, a, b, start, stop, r):
+        bk = "pb%d" % bank
+        return op("P", lambda: P.matmul_mx(T[bk][:, 0:b - a], lq[:, 128 * k:128 * k + 128], ls[:, 128 * k:128 * k + 128],
+                                           rq[:, a:b], rs[:, a:b], start, stop), r=r, w=[bk])
+
+    def ms(out, val, w):
+        return op("V", lambda: V.memset(out, val), w=w)
+
+    def ts(out, in0, s1, s2, o0, o1, r, w, x=()):
+        if o1 is None:
+            return op("V", lambda: V.tensor_scalar(out, in0, s1, None, o0), r=r, w=w, x=x)
+        return op("V", lambda: V.tensor_scalar(out, in0, s1, s2, o0, o1), r=r, w=w, x=x)
+
+    def tt(out, in0, in1, o, r, w, x=()):
+        return op("V", lambda: V.tensor_tensor(out, in0, in1, o), r=r, w=w, x=x)
+
+    def cp(out, in_, r, w, x=()):
+        return op("V", lambda: V.tensor_copy(out, in_), r=r, w=w, x=x)
+
+    def scan(out, d0, d1, o0, o1, r, w):
+        return op("V", lambda: V.tensor_tensor_scan(out, d0, d1, 0.0, o0, o1), r=r, w=w)
+
+    def turn(out, in_, r, w):
+        return op("V", lambda: V.transpose(out, in_), r=r, w=w)
+
+    def act(out, in_, f, r, w, x=(), **kw):
+        return op("A", lambda: S_.activation(out, in_, f, **kw), r=r, w=w, x=x)
+
+    def iota(out, pat, base, cm, w, small=False):
+        if small:
+            return op("G", lambda: g.iota(out, pat, base, cm, allow_small_or_imprecise_dtypes=True), w=w)
+        return op("G", lambda: g.iota(out, pat, base, cm), w=w)
+
+    def dma(q, out, in_, sem, r=(), w=()):
+        return op(q, lambda: Q[q].dma_start(out, in_), r=r, w=w, sem=sem, inc=16)
+
+    NENG = min(len(topo.engines(a, b)) for a in T.cores for b in T.cores if a != b)
+
+    def send(dst, out, in_, rsem, r):
+        for key in r:
+            wait("G", writer[key])
+        rid, pid, _e = topo.addr(dst)
+        eng = topo.engines(core, dst)[:NENG]
+        g.remote_dma(out, in_, T.sem[rsem], T.sem.left, pid, rid, sum(1 << e for e in eng))
+        count["left"] = count.get("left", 0) + len(eng)
+
+    dma("S", T.xt[:], T.x[:], "d0", w=["xt"])
+    dma("A", T.ut[:], T.u[:], "d1", w=["ut"])
+    for G in range(8):
+        s = 20 * (G & 1) + 10 * (G >> 1 & 1) + 5 * (G >> 2)
+        dma("S", T.cdl[16 * G:16 * G + 16, 0:445], T.cd[:, s:s + 445], "d2", w=["cdl%d" % G])
+    writer["cdl"] = ("d2", count["d2"])
+    dma("S", T.wq[:].bitcast(dt.uint8), T.wc[:], "d3", w=["wq"])
+    dma("S", T.wsc[:], T.ws[:], "d3", w=["wsc"])
+    writer["wq"] = writer["wsc"]
+    dma("S", T.vt[:], T.v[:], "d4", w=["vt"])
+
+    OFFJ = [256 * 16 * n - 512 for n in NA]
+    ms(T.ones[:], 1.0, ["ones"])
+    iota(T.ip[:], [[0, 2]], 0, 1, ["ip"])
+    iota(T.li[:, 0:8], [[16, 8]], 0, 0, ["li_u"])
+    op("G", lambda: g.affine_select(T.ident[:], T.ones[:], [[-1, 128]], A.is_equal, 0.0, 0, 1), r=["ones"], w=["ident"])
+    iota(T.cmi[:], [[0, 16], [1, 8], [0, 4]], 0, 0, ["cmi"], True)
+    iota(T.i16[:], [[0, 20], [1, 16]], 0, 0, ["i16"], True)
+    iota(T.ij[:], [[H + OFFJ[1] - OFFJ[0], 2], [1, H]], OFFJ[0], 0, ["ij"], True)
+    for i, pat in enumerate(([[0, 2], [1, 2], [0, 8]], [[1, 2], [2, 2], [0, 8]], [[0, 2], [16, 2], [1, 8]],
+                             [[0, 4], [160, 4], [16, 2]], [[0, 4], [20, 2], [1, 4]], [[0, 4], [80, 4], [8, 2]])):
+        iota(T.fi[:, 32 * i:32 * i + 32], pat, 0, 0, ["fi%d" % i], True)
+    for name, pat, base in (("own", [[16, 5], [0, 2]], 0), ("cmp", [[4, 2], [32, 5], [2, 2]], 0), ("bad", [[32, 20]], 0),
+                            ("sel", [[4, 2], [32, 5]], 0), ("w", [[0, 4], [4, 5]], 0), ("v", [[0, 2], [16, 5]], 7),
+                            ("uu", [[20, 2], [4, 5]], 40)):
+        c0, n = LISTS[name]
+        iota(T.li[:, c0:c0 + n], pat, base, 0, ["li_" + name])
+    iota(T.ic[:], [[1, C]], 0, 0, ["ic"], True)
+
+    def bf(i):
+        return T.bf[:, i:i + 1]
+
+    def cf(i):
+        return T.cf[:, i:i + 1]
+
+    def fo(i):
+        return T.fo[:, 32 * i:32 * i + 1]
+
+    ms(T.warm[:], 0.0, ["warm"])
+    ms(T.keep[:], 1.0, ["keep"])
+    ms(T.rmin[:], -2.0 ** 30, ["rmin"])
+    act(T.warm[:, 1:2], T.warm[:, 0:1], AF.Exp, ["warm"], ["warm1"])
+    for i, m in enumerate((15, 32, 64, 7)):
+        ts(T.bi[:, i:i + 1], T.ip[:, 0:1], m, None, A.bitwise_and, None, ["ip"], ["bi%d" % i])
+    ts(T.bi[:, 4:5], T.ip[:, 0:1], 4, None, A.arith_shift_right, None, ["ip"], ["bi4"])
+    cp(T.lu[:, 0:8], T.li[:, 0:8], ["li_u"], ["lu_u"])
+    ms(T.keep[:, 0:C:8], 0.0, ["keep"])
+    ms(T.rmin[:, 0:160:8], 2.0 ** 30, ["rmin"])
+    cp(T.bf[:, 0:5], T.bi[:, 0:5], ["bi%d" % i for i in range(5)], ["bf"])
+    zeros = {1: ["z12", "z13"], 5: ["z51", "z52", "z53"]}
+    ms(T.ft1[:, 2:4 * H:4], 0.0, ["z12"])
+    ms(T.ft1[:, 3:4 * H:4], 0.0, ["z13"])
+    ms(T.ft5[:, 4 * H + 1:4 * C:4], 0.0, ["z51"])
+    ms(T.ft5[:, 4 * H + 2:4 * C:4], 0.0, ["z52"])
+    ms(T.ft5[:, 3:4 * C:4], 0.0, ["z53"])
+    ms(T.ft4[:, 0:4 * H], 0.0, ["z4"])
+    ts(cf(0), bf(1), 5.0, bf(0), A.mult, A.add, ["bf"], ["cf0"])
+    ts(cf(1), bf(2), 1.25, None, A.mult, None, ["bf"], ["cf1"])
+    ts(cf(2), bf(3), 0.0625, None, A.mult, None, ["bf"], ["cf2"])
+    ts(cf(3), bf(0), -2.0 ** 90, None, A.mult, None, ["bf"], ["cf3"])
+    quant(T.fq4, T.fs4, T.ft4, 0, H, ["z4"], ["fq4_0"])
+    for b in range(4):
+        for e in range(4):
+            act(T.et[:, 512 * b + e:512 * b + 512:4], T.ident[:], AF.Identity, ["ident"], ["et%d%d" % (b, e)],
+                scale=1.0 if b == e else 0.0)
+    act(T.negm[:], T.i16[:], AF.Abs, ["i16", "cf3"], ["negm"], scale=2.0 ** 90, bias=cf(3))
+    act(T.rst[:], T.i16[:], AF.Identity, ["i16"], ["rst"], scale=2.0 ** 96, bias=-2.0 ** 95)
+    act(T.ijg[:], T.ij[:], AF.Identity, ["ij", "cf2"], ["ijg"], bias=cf(2))
+    ts(T.ct[:, 0:512], T.cmi[:], bf(4), 512.0, A.is_equal, A.mult, ["cmi", "bf"], ["ct0"])
+    ts(T.ct[:, 512:1024], T.cmi[:], bf(4), 256.0, A.is_equal, A.mult, ["cmi", "bf"], ["ct1"])
+    quant(T.uq, T.us, T.ut, 0, 128, ["ut"], ["uq"])
+    quant(T.tq0, T.ts0, T.xt, 0, C, ["xt"], ["tq0_0", "tq0_1"])
+    cp(T.urq[:].bitcast(dt.uint32), T.uq[:].bitcast(dt.uint32).indirect(lst("u")), ["uq", "lu_u"], ["urq"])
+    cp(T.urs[:], T.us[:].indirect(lst("u")), ["uq", "lu_u"], ["urs"])
+    quant(T.cq, T.cs, T.ct, 0, 256, ["ct0", "ct1"], ["cq"])
+
+    def late_constants():
+        quant(T.eq, T.es, T.et, 0, 512, ["et%d%d" % (b, e) for b in range(4) for e in range(4)], ["eq"])
+        turn(T.fo[:], T.fi[:], ["fi%d" % i for i in range(6)], ["fo"])
+
+    def lists(names):
+        for name, c1, c2 in (("own", cf(0), cf(1)), ("cmp", fo(0), None), ("bad", fo(2), None), ("sel", fo(1), fo(3)),
+                             ("w", fo(4), None), ("v", fo(5), None), ("uu", fo(1), None)):
+            if name in names:
+                c0, n = LISTS[name]
+                ts(T.lu[:, c0:c0 + n], T.li[:, c0:c0 + n], c1, c2, A.add, None if c2 is None else A.add,
+                   ["li_" + name, "fo", "cf0", "cf1"], ["lu_" + name])
+
+    def candidates():
+        for sl in range(5):
+            for g2 in range(2):
+                cp(T.cdu[:, 2 * sl + g2:120:10], T.cdl[:, sl:sl + 441:40], ["cdl"], ["cdu%d" % (2 * sl + g2)])
+
+    cdu_keys = ["cdu%d" % i for i in range(10)]
+    LN2 = math.log(2.0)
+    MAGIC = 1.5 * 2.0 ** 41
+
+    def scores(t, h):
+        for bank in (SV[h], SA[h]):
+            mm(bank, T.urq, T.urs, 0, T["tq%d" % t], T["ts%d" % t], H * h, H * h + H, True, True,
+               ["urq", "urs", "tq%d_%d" % (t, h)])
+
+    def own_scores(h):
+        lo, hi, bk = H * h, H * h + H, "pb%d" % SV[h]
+        tt(T.pm[:, lo:hi], T[bk][:, 0:H], T.negm[:, lo:hi], A.subtract, ["negm"], ["pm%d" % h], x=[bk])
+
+    def own_scan(h):
+        lo, hi = H * h, H * h + H
+        scan(T.th[:, lo:hi], T.rst[:, lo:hi], T.pm[:, lo:hi], A.min, A.max, ["rst", "pm%d" % h], ["th%d" % h])
+
+    def ties(h):
+        lo, bk = H * h, "pb%d" % SV[h]
+        tt(T.ft0[:, 4 * lo:4 * lo + 4 * H:4], T[bk][:, 0:H], T.th[:, lo:lo + H], A.is_equal, ["th%d" % h],
+           ["f0_0_%dl" % h], x=[bk])
+
+    def cut(m, h):
+        return min(max(16 * m + 16 - H * h, 0), H)
+
+    def vrow(m, h, f, e):
+        ft, c, lo, sc, bk = T["ft%d" % f], cut(m, h), H * h, T.th[:, 16 * m + 15:16 * m + 16], "pb%d" % SV[h]
+        k, o = (None, None) if f < 3 else (2.0, A.mult)
+        if c > 0:
+            ts(ft[:, 4 * lo + e:4 * (lo + c):4], T[bk][:, 0:c], sc, k, A.is_lt, o, ["th%d" % (m // 10)],
+               ["f%d_%d_%dl" % (f, e, h)], x=[bk])
+        if c < H:
+            ts(ft[:, 4 * (lo + c) + e:4 * (lo + H):4], T[bk][:, c:H], sc, k, A.is_le, o, ["th%d" % (m // 10)],
+               ["f%d_%d_%dr" % (f, e, h)], x=[bk])
+
+    def arows(rows, base):
+        def one(i):
+            m, h, f, e = rows[i]
+            k, bk = base + i, "pb%d" % SA[h]
+            act(T.sg[:, H * k:H * k + H], T[bk][:, 0:H], AF.Sign, ["th%d" % (m // 10)], ["sg%d" % k], x=[bk],
+                bias=T.th[:, 16 * m + 15:16 * m + 16], scale=-1.0)
+
+        def two(i):
+            m, h, f, e = rows[i]
+            k = base + i
+            ft, c, lo = T["ft%d" % f], cut(m, h), H * h
+            if c > 0:
+                act(ft[:, 4 * lo + e:4 * (lo + c):4], T.sg[:, H * k:H * k + c], AF.Sign, ["sg%d" % k],
+                    ["f%d_%d_%dl" % (f, e, h)], bias=-0.5)
+            if c < H:
+                act(ft[:, 4 * (lo + c) + e:4 * (lo + H):4], T.sg[:, H * k + c:H * k + H], AF.Sign, ["sg%d" % k],
+                    ["f%d_%d_%dr" % (f, e, h)], bias=0.5)
+        one(0)
+        for i in range(len(rows)):
+            if i + 1 < len(rows):
+                one(i + 1)
+            two(i)
+
+    def qflags(f, halves):
+        keys = ["f%d_%d_%d%s" % (f, e, h, s) for e in range(4) for h in halves for s in "lr"] + zeros.get(f, [])
+        quant(T["fq%d" % f], T["fs%d" % f], T["ft%d" % f], H * halves[0], H * halves[-1] + H, keys,
+              ["fq%d_%d" % (f, h) for h in halves])
+
+    def tally(f, n=C):
+        mm(CNT, T.cq, T.cs, 0 if f < 3 else 1, T["fq%d" % f], T["fs%d" % f], 0, n, f == 0, f == 6,
+           ["cq", "fq%d_0" % f, "fq%d_1" % f])
+
+    def early(t):
+        scores(t, 0)
+        own_scores(0)
+        own_scan(0)
+        arows([(9, 0, 3, 0), (8, 0, 3, 1), (7, 0, 3, 2), (6, 0, 3, 3), (0, 0, 5, 1)], 0)
+        ties(0)
+        for i, m in enumerate((1, 2, 3, 4, 5)):
+            vrow(m, 0, (i + 1) // 4, (i + 1) % 4)
+            if i == 3:
+                qflags(0, [0])
+        qflags(1, [0])
+
+    early(0)
+    late_constants()
+
+    for t in range(R):
+        donor = T.cores[(rank + 1 + t) % N]
+        child = T.cores[(rank - 1 - t) % N]
+        tq, tsc, tk = T["tq%d" % t], T["ts%d" % t], ["tq%d_0" % t, "tq%d_1" % t]
+
+        def unpack(b):
+            mm(DTB[b], T.eq, T.es, b, tq, tsc, 0, C, True, True, ["eq"] + tk)
+
+        def window(b):
+            bk = "pb%d" % DTB[b]
+            act(T.dtw[:, C * b:C * b + C], T[bk][:, 0:C], AF.Copy, [], ["dtw%d" % b], x=[bk])
+
+        scores(t, 1)
+        for b in range(3):
+            unpack(b)
+        qflags(3, [0])
+        own_scores(1)
+        vrow(9, 1, 2, 3)
+        own_scan(1)
+        arows([(0, 1, 3, 0), (1, 1, 3, 1), (2, 1, 3, 2), (3, 1, 3, 3), (4, 1, 5, 0), (14, 0, 5, 0), (15, 0, 5, 2),
+               (5, 1, 4, 0), (6, 1, 4, 1), (7, 1, 4, 2), (8, 1, 4, 3),
+               (16, 0, 6, 0), (17, 0, 6, 1), (18, 0, 6, 2)], 5)
+        if t == 0:
+            lists(("own", "cmp"))
+        ties(1)
+        for m in range(10, 14):
+            vrow(m, 1, (m - 9) // 4, (m - 9) % 4)
+        qflags(0, [1])
+        tally(0)
+        for m in range(14, 18):
+            vrow(m, 1, (m - 9) // 4, (m - 9) % 4)
+        qflags(1, [1])
+        tally(1)
+        qflags(3, [1])
+        tally(3)
+        vrow(18, 1, 2, 1)
+        vrow(19, 1, 2, 2)
+        for m in range(10, 14):
+            vrow(m, 0, 2, m - 10)
+        qflags(5, [0, 1])
+        tally(5)
+        vrow(19, 0, 6, 3)
+        qflags(2, [0, 1])
+        tally(2)
+        qflags(4, [1])
+        tally(4)
+        qflags(6, [0])
+        tally(6, H)
+        unpack(3)
+        if t == 0:
+            candidates()
+        window(0)
+        window(1)
+
+        tt(T.pcw[:], T["pb%d" % CNT][:, 0:C], T.ijg[:], A.add, ["ijg"], ["pcw"], x=["pb%d" % CNT])
+        cp(T.gk[:], T.pcw[:].indirect(lst("own")), ["pcw", "lu_own"], ["gk"])
+        for h in range(2):
+            act(T.gc1[:, C * h:C * h + C], T.pcw[:].indirect(T.cdu[:, 40 * t + 20 * h:40 * t + 20 * h + 20]), AF.Copy,
+                ["pcw"] + cdu_keys, ["gc%d" % h])
+        turn(T.tk[:, 0:160], T.gk[:], ["gk"], ["tk"])
+        turn(T.tk[:, 160:C], T.gk[:], ["gk"], ["tk2"])
+        for h in range(2):
+            tt(T.fl[:, 160 * h:160 * h + 160], T.tk[:, 160:C].indirect(lst("cmp", 10 * h, 10 * h + 10)), T.tk[:, 0:160],
+               A.is_gt, ["tk", "tk2", "lu_cmp"], ["fl%d" % h])
+        scan(T.ps[:], T.keep[:], T.fl[:], A.mult, A.add, ["keep", "fl0", "fl1"], ["ps"])
+        wo, wl = T["wo%d" % t], T["wl%d" % t]
+        act(wo[:, 0:40], T.ps[:, 7:C:8], AF.Exp, ["ps"], ["wo0"], scale=-LN2, bias=7 * LN2)
+        cp(wo[:, 40:80], T.ps[:, 7:C:8], ["ps"], ["wo1"])
+        send(donor, wl[:], wo[:], "wa%d" % t, ["wo0", "wo1"])
+
+        if t == 0:
+            lists(("bad", "sel", "w", "v", "uu"))
+        turn(T.tg[:, 0:C], T.gc1[:, 0:C], ["gc0"], ["tg0"])
+        turn(T.tg[:, C:2 * C], T.gc1[:, C:2 * C], ["gc1"], ["tg1"])
+        window(2)
+        tgk = ["tg0", "tg1"]
+        thr = 512.0 * TH
+        act(T.sb[:, 0:160], T.tg[:].indirect(lst("sel")), AF.Sign, tgk + ["lu_sel"], ["sb"], bias=0.25 - thr)
+        act(T.sb[:, 160:C], T.sb[:, 0:160], AF.Identity, ["sb"], ["tt"], scale=-2.0 ** 17, bias=-2.0 ** 17)
+        ts(T.bad[:], T.tg[:].indirect(lst("bad")), thr, None, A.is_ge, None, tgk + ["lu_bad"], ["bad"])
+
+        arrives("wl", "wa%d" % t, NENG)
+        act(T.ub[:], wl[:].indirect(lst("uu")), AF.Exp, ["wl", "lu_uu"], ["ub"], scale=LN2,
+            bias=10 * LN2 + math.log(1.0 + 2.0 ** -9))
+        window(3)
+        tt(T.pc2[:], T.tg[:].indirect(lst("sel")), T.sb[:, 160:C], A.add, tgk + ["lu_sel", "tt"], ["pc2"])
+        tt(T.dd[:], wl[:].indirect(lst("w")), T.bad[:], A.mult, ["wl", "lu_w", "bad"], ["dd"])
+        scan(T.vv[:], T.keep[:], T.dd[:], A.mult, A.add, ["keep", "dd"], ["vv"])
+        yy, zz, ky = T.yy[:, 0:160], T.yy[:, 160:320], T.yy[:, 320:480]
+        tt(yy, T.vv[:].indirect(lst("v")), T.ub[:], A.mult, ["vv", "lu_v", "ub"], ["yy"])
+        ts(zz, yy, MAGIC, -(MAGIC + 2.0 ** 24), A.add, A.add, ["yy"], ["zz"])
+        tt(ky, zz, T.pc2[:], A.add, ["zz", "pc2"], ["ky"])
+        scan(T.mn[:], T.rmin[:], ky, A.max, A.min, ["rmin", "ky"], ["mn"])
+        for a1 in range(2):
+            for b1 in range(2):
+                cp(T.e1[64 * b1:64 * b1 + 64, 10 * a1:10 * a1 + 10], T.mn[64 * a1:64 * a1 + 64, 80 * b1 + 7:80 * b1 + 80:8],
+                   ["mn"], ["e1_%d%d" % (a1, b1)])
+        ts(T.e1[:, 20:40], T.e1[:, 0:20], 511, None, A.bitwise_and, None, ["e1_00", "e1_01", "e1_10", "e1_11"], ["e2"])
+        eok = [["eo%d%d" % (h, i) for i in range(4)] for h in range(2)]
+
+        def leaders(a0):
+            for b1 in range(2):
+                for b0 in range(2):
+                    src, dst = 64 * b1 + 32 * a0, 64 * b1 + 32 * b0
+                    cp(T.eo[dst:dst + 32, 10 * a0:10 * a0 + 10], T.e1[src:src + 32, 20 + b0:40:2], ["e2"],
+                       [eok[a0][2 * b1 + b0]])
+
+        zq, zs, hq, hs, lq, ls = (T["%s%d" % (n, t)] for n in ("zq", "zs", "hq", "hs", "lq", "ls"))
+        banks = ((3, 4, 5, 6), (0, 1, 2, 7))
+
+        def part(h, b, q):
+            out, win = T.zt[:, 4 * H * h + b:4 * H * (h + 1):4], T.dtw[:, C * b:C * b + C].indirect(T.eo[:, 10 * h:10 * h + 10])
+            if q == "V":
+                cp(out, win, ["dtw%d" % b] + eok[h], ["zt%d%d" % (b, h)])
+            else:
+                act(out, win, AF.Copy, ["dtw%d" % b] + eok[h], ["zt%d%d" % (b, h)])
+
+        def layer(h):
+            quant(zq, zs, T.zt, H * h, H * h + H, ["zt%d%d" % (b, h) for b in range(4)], ["zq%d" % h])
+            for b in range(4):
+                mm(banks[h][b], T.wq, T.wsc, b, zq, zs, H * h, H * h + H, True, True, ["wq", "zq%d" % h])
+
+        def relu(h, b, q):
+            bk, out = "pb%d" % banks[h][b], T.ht[:, 4 * H * h + b:4 * H * (h + 1):4]
+            if q == "V":
+                ts(out, T[bk][:, 0:H], 0.0, 0.015625, A.max, A.mult, [], ["ht%d%d" % (b, h)], x=[bk])
+            else:
+                act(out, T[bk][:, 0:H], AF.Relu, [], ["ht%d%d" % (b, h)], x=[bk], scale=0.015625)
+
+        def ship(h):
+            lo, hi = H * h, H * h + H
+            quant(hq, hs, T.ht, lo, hi, ["ht%d%d" % (b, h) for b in range(4)], ["hq%d" % h])
+            send(child, lq[:, lo:hi].bitcast(dt.uint8), hq[:, lo:hi].bitcast(dt.uint8), "ha%d" % (2 * t + h), ["hq%d" % h])
+            send(child, ls[:, lo:hi], hs[:, lo:hi], "ha%d" % (2 * t + h), ["hq%d" % h])
+        leaders(0)
+        for b in range(4):
+            part(0, b, "VA"[b % 2])
+        layer(0)
+        leaders(1)
+        for b in range(4):
+            part(1, b, "A")
+            relu(0, b, "V")
+        ship(0)
+        layer(1)
+        if t == R - 1:
+            ts(T.elb[:], T.ic[:].indirect(T.eo[:]), 0.0, None, A.add, None, ["ic"] + eok[0] + eok[1], ["elb"])
+            dma("S", T.el[:], T.elb[0:128:16, :], "d5", r=["elb"])
+        for b in range(4):
+            relu(1, b, "AV"[b % 2])
+        ship(1)
+        if t == 0:
+            quant(T.vq, T.vs, T.vt, 0, 128, ["vt"], ["vq"])
+
+        nq, ns = T["tq%d" % (t + 1)], T["ts%d" % (t + 1)]
+        for h in range(2):
+            lo, hi = H * h, H * h + H
+            for b in range(4):
+                mm(3 + b, T.eq, T.es, b, tq, tsc, lo, hi, True, False, ["eq"] + tk)
+            arrives("lq%d" % h, "ha%d" % (2 * t + h), 2 * NENG)
+            for b in range(4):
+                bk, out = "pb%d" % (3 + b), T.xn[:, 4 * lo + b:4 * hi:4]
+                mm(3 + b, T.eq, T.es, b, lq, ls, lo, hi, False, True, ["eq", "lq%d" % h])
+                if ("AVVV" if h == 1 and t + 1 < R else "AVAV")[b] == "V":
+                    cp(out, T[bk][:, 0:H], [], ["xn%d%d" % (b, h)], x=[bk])
+                else:
+                    act(out, T[bk][:, 0:H], AF.Copy, [], ["xn%d%d" % (b, h)], x=[bk])
+            quant(nq, ns, T.xn, lo, hi, ["xn%d%d" % (b, h) for b in range(4)], ["tq%d_%d" % (t + 1, h)])
+            if t + 1 < R:
+                if h == 0:
+                    early(t + 1)
+            else:
+                key = "tq%d_%d" % (R, h)
+                mm(h, T.vq, T.vs, 0, nq, ns, lo, hi, True, True, ["vq", key])
+                dma("S", T.oc[:, 4 * lo:4 * hi], nq[:, lo:hi].bitcast(dt.uint8), "d%d" % (6 + h), r=[key])
+                cp(T.yb[:, lo:hi], T["pb%d" % h][:, 0:H], [], ["yb%d" % h], x=["pb%d" % h])
+                if h == 1:
+                    for k in range(4):
+                        dma("A" if k % 2 else "S", T.osc[4 * k:4 * k + 4, :], ns[32 * k:32 * k + 4, :], "d10",
+                            r=["tq%d_0" % R, key])
+                dma("S" if h == 0 else "A", T.y[:, lo:hi], T.yb[:, lo:hi], "d%d" % (8 + h), r=["yb%d" % h])
+
+    for sem in sorted(count):
+        wait("G", (sem, count[sem]))

@@ -2,8 +2,15 @@ import math
 from concourse.mybir import dt, AluOpType, ActivationFunctionType
 
 C, TH, R, N = 320, 240, 3, 8
-H = C // 2
-NA = (10, 9)
+CUT = 192
+CH = ((0, CUT), (CUT, C))
+SLOT = (0, 128, CUT)
+VEARLY = (0, 4, 8)
+AEARLY = (1, 2, 3)
+ALATE = (1, 2, 3, 5, 6, 7, 9, 10, 11, 13)
+XN = ("AVAV", "AVAV")
+LAG = 600
+LATE1 = 0
 F32, BF, I32, U16, Q4, U8 = "float32", "bfloat16", "int32", "uint16", "float8_e4m3fn_x4", "uint8"
 
 
@@ -12,23 +19,23 @@ def _s(n, d):
 
 
 SCRATCH = {
-    "xt": _s(4 * C, BF), "ut": _s(512, BF), "vt": _s(512, BF), "cdl": _s(448, I32),
+    "xt": _s(4 * C, BF), "ut": _s(512, BF), "vt": _s(512, BF), "cdl": _s(456, I32),
     "uq": _s(128, Q4), "us": _s(128, U8), "urq": _s(128, Q4), "urs": _s(128, U8), "vq": _s(128, Q4), "vs": _s(128, U8),
     "wq": _s(512, Q4), "wsc": _s(512, U8),
-    "ones": _s(128, BF), "ident": _s(128, BF), "et": _s(2048, BF), "eq": _s(512, Q4), "es": _s(512, U8),
-    "cmi": _s(512, BF), "ct": _s(1024, BF), "cq": _s(256, Q4), "cs": _s(256, U8),
-    "ip": _s(2, I32), "bi": _s(8, I32), "bf": _s(8, F32), "cf": _s(4, F32), "fi": _s(192, F32), "fo": _s(192, F32),
-    "li": _s(112, I32), "lu": _s(112, U16), "cdu": _s(120, U16),
-    "i16": _s(C, F32), "ij": _s(C, F32), "ijg": _s(C, F32), "ic": _s(C, F32), "negm": _s(C, F32), "rst": _s(C, F32),
-    "keep": _s(C, BF), "rmin": _s(160, F32), "warm": _s(2, F32),
-    "pm": _s(C, F32), "th": _s(C, F32), "sg": _s(sum(NA) * H, BF),
-    "gk": _s(160, F32), "tk": _s(C, F32), "fl": _s(C, BF), "ps": _s(C, BF),
-    "pcw": _s(C, F32), "gc1": _s(640, F32), "tg": _s(640, F32), "bad": _s(C, BF), "sb": _s(C, F32), "pc2": _s(160, I32),
-    "ub": _s(160, F32), "dd": _s(C, BF), "vv": _s(C, BF), "yy": _s(480, F32),
-    "mn": _s(160, F32), "e1": _s(40, I32), "eo": _s(20, U16), "elb": _s(C, F32),
+    "et": _s(1032, BF), "eq": _s(512, Q4), "es": _s(512, U8),
+    "cmi": _s(512, BF), "ct": _s(512, BF), "cq": _s(128, Q4), "cs": _s(128, U8),
+    "dgi": _s(512, BF), "dtl": _s(1024, BF), "dq": _s(256, Q4), "ds": _s(256, U8), "tb": _s(192, F32),
+    "ip": _s(2, I32), "bi": _s(4, I32), "bf": _s(4, F32), "cf": _s(8, F32), "fi": _s(224, F32), "fo": _s(224, F32),
+    "li": _s(56, I32), "lu": _s(60, U16), "cdu": _s(72, U16),
+    "i16": _s(CUT, F32), "ij": _s(C, F32), "ic": _s(C, F32), "negm": _s(CUT, F32), "rst": _s(CUT, F32),
+    "keep": _s(192, BF), "rmin": _s(128, F32), "warm": _s(2, F32),
+    "pm": _s(C, F32), "th": _s(C, F32), "sg": _s(4 * C, BF), "fl": _s(192, BF), "ps": _s(192, BF),
+    "pcw": _s(C, F32), "gc1": _s(384, F32), "tg": _s(384, F32), "bad": _s(192, BF), "pc2": _s(192, F32),
+    "ub": _s(192, F32), "dd": _s(192, BF), "vv": _s(192, BF), "yy": _s(576, F32),
+    "mn": _s(288, F32), "rb": _s(128, F32), "ci": _s(72, I32), "cj": _s(144, I32), "eo": _s(32, U16), "elb": _s(C, F32),
     "dtw": _s(4 * C, BF), "zt": _s(4 * C, BF), "ht": _s(4 * C, BF), "xn": _s(4 * C, BF), "yb": _s(C, F32),
 }
-for _i in range(7):
+for _i in range(6):
     SCRATCH["ft%d" % _i] = _s(4 * C, BF)
     SCRATCH["fq%d" % _i] = _s(C, Q4)
     SCRATCH["fs%d" % _i] = _s(C, U8)
@@ -39,17 +46,17 @@ for _i in range(R):
     for _n in ("z", "h", "l"):
         SCRATCH["%sq%d" % (_n, _i)] = _s(C, Q4)
         SCRATCH["%ss%d" % (_n, _i)] = _s(C, U8)
-    SCRATCH["wo%d" % _i] = _s(80, BF)
-    SCRATCH["wl%d" % _i] = _s(80, BF)
+    SCRATCH["wo%d" % _i] = _s(48, BF)
+    SCRATCH["wl%d" % _i] = _s(48, BF)
 for _i in range(8):
     SCRATCH["pb%d" % _i] = ("psum", [128, 512], F32)
 
 SEMAPHORES = (["cV", "cA", "cP", "cG", "left"] + ["wa%d" % i for i in range(R)] + ["ha%d" % i for i in range(2 * R)]
-              + ["d%d" % i for i in range(12)])
+              + ["d%d" % i for i in range(16)])
 
-LISTS = {"u": (0, 8), "own": (8, 10), "cmp": (18, 20), "bad": (38, 20), "sel": (58, 10), "w": (68, 20), "v": (88, 10),
-         "uu": (98, 10)}
-SV, SA, CNT, DTB = (0, 2), (1, 7), 5, (3, 4, 6, 0)
+LISTS = {"w": 8, "v": 20, "uu": 32, "pc": 44}
+UB, SV, SA, DB, CNT = (0, 1, 2, 3), 4, 5, 6, 7
+VB, AB = (CNT, SV), (SA, UB[0])
 
 
 def rank_program(g, core, T, topo):
@@ -108,16 +115,20 @@ def rank_program(g, core, T, topo):
 
     V, S_, P = g.vector, g.scalar, g.tensor
 
-    def lst(name, a=0, b=None):
-        c0, n = LISTS[name]
-        return T.lu[:, c0 + a:c0 + (n if b is None else b)]
+    def lst(name, k):
+        c0 = LISTS[name] + 8 * k
+        return T.lu[:, c0:c0 + 8 - 4 * k]
 
-    def quant(qb, sb, tb, a, b, r, w):
-        return op("V", lambda: V.quantize_mx(qb[:, a:b], sb[:, a:b], tb[:, 4 * a:4 * b]), r=r, w=w)
+    def keys(name, a, b):
+        return ["%s_%d" % (name, k) for k, (lo, hi) in enumerate(CH) if lo < b and a < hi]
 
-    def mm(bank, lq, ls, k, rq, rs, a, b, start, stop, r):
+    def quant(qb, sb, tb, a, b, r, w, at=None):
+        at = 4 * a if at is None else at
+        return op("V", lambda: V.quantize_mx(qb[:, a:b], sb[:, a:b], tb[:, at:at + 4 * (b - a)]), r=r, w=w)
+
+    def mm(bank, lq, ls, c, rq, rs, a, b, start, stop, r):
         bk = "pb%d" % bank
-        return op("P", lambda: P.matmul_mx(T[bk][:, 0:b - a], lq[:, 128 * k:128 * k + 128], ls[:, 128 * k:128 * k + 128],
+        return op("P", lambda: P.matmul_mx(T[bk][:, 0:b - a], lq[:, c:c + 128], ls[:, c:c + 128],
                                            rq[:, a:b], rs[:, a:b], start, stop), r=r, w=[bk])
 
     def ms(out, val, w):
@@ -131,9 +142,6 @@ def rank_program(g, core, T, topo):
     def tt(out, in0, in1, o, r, w, x=()):
         return op("V", lambda: V.tensor_tensor(out, in0, in1, o), r=r, w=w, x=x)
 
-    def cp(out, in_, r, w, x=()):
-        return op("V", lambda: V.tensor_copy(out, in_), r=r, w=w, x=x)
-
     def scan(out, d0, d1, o0, o1, r, w):
         return op("V", lambda: V.tensor_tensor_scan(out, d0, d1, 0.0, o0, o1), r=r, w=w)
 
@@ -142,6 +150,11 @@ def rank_program(g, core, T, topo):
 
     def act(out, in_, f, r, w, x=(), **kw):
         return op("A", lambda: S_.activation(out, in_, f, **kw), r=r, w=w, x=x)
+
+    def cp(out, in_, r, w, x=(), q="V"):
+        if q == "A":
+            return act(out, in_, AF.Copy, r, w, x)
+        return op("V", lambda: V.tensor_copy(out, in_), r=r, w=w, x=x)
 
     def iota(out, pat, base, cm, w, small=False):
         if small:
@@ -161,34 +174,23 @@ def rank_program(g, core, T, topo):
         g.remote_dma(out, in_, T.sem[rsem], T.sem.left, pid, rid, sum(1 << e for e in eng))
         count["left"] = count.get("left", 0) + len(eng)
 
-    dma("S", T.xt[:], T.x[:], "d0", w=["xt"])
-    dma("A", T.ut[:], T.u[:], "d1", w=["ut"])
-    for G in range(8):
-        s = 20 * (G & 1) + 10 * (G >> 1 & 1) + 5 * (G >> 2)
-        dma("S", T.cdl[16 * G:16 * G + 16, 0:445], T.cd[:, s:s + 445], "d2", w=["cdl%d" % G])
-    writer["cdl"] = ("d2", count["d2"])
-    dma("S", T.wq[:].bitcast(dt.uint8), T.wc[:], "d3", w=["wq"])
-    dma("S", T.wsc[:], T.ws[:], "d3", w=["wsc"])
-    writer["wq"] = writer["wsc"]
-    dma("S", T.vt[:], T.v[:], "d4", w=["vt"])
+    def weave(*chains):
+        for i in range(max(len(c) for c in chains)):
+            for c in chains:
+                if i < len(c) and c[i] is not None:
+                    c[i]()
 
-    OFFJ = [256 * 16 * n - 512 for n in NA]
-    ms(T.ones[:], 1.0, ["ones"])
-    iota(T.ip[:], [[0, 2]], 0, 1, ["ip"])
-    iota(T.li[:, 0:8], [[16, 8]], 0, 0, ["li_u"])
-    op("G", lambda: g.affine_select(T.ident[:], T.ones[:], [[-1, 128]], A.is_equal, 0.0, 0, 1), r=["ones"], w=["ident"])
-    iota(T.cmi[:], [[0, 16], [1, 8], [0, 4]], 0, 0, ["cmi"], True)
-    iota(T.i16[:], [[0, 20], [1, 16]], 0, 0, ["i16"], True)
-    iota(T.ij[:], [[H + OFFJ[1] - OFFJ[0], 2], [1, H]], OFFJ[0], 0, ["ij"], True)
-    for i, pat in enumerate(([[0, 2], [1, 2], [0, 8]], [[1, 2], [2, 2], [0, 8]], [[0, 2], [16, 2], [1, 8]],
-                             [[0, 4], [160, 4], [16, 2]], [[0, 4], [20, 2], [1, 4]], [[0, 4], [80, 4], [8, 2]])):
-        iota(T.fi[:, 32 * i:32 * i + 32], pat, 0, 0, ["fi%d" % i], True)
-    for name, pat, base in (("own", [[16, 5], [0, 2]], 0), ("cmp", [[4, 2], [32, 5], [2, 2]], 0), ("bad", [[32, 20]], 0),
-                            ("sel", [[4, 2], [32, 5]], 0), ("w", [[0, 4], [4, 5]], 0), ("v", [[0, 2], [16, 5]], 7),
-                            ("uu", [[20, 2], [4, 5]], 40)):
-        c0, n = LISTS[name]
-        iota(T.li[:, c0:c0 + n], pat, base, 0, ["li_" + name])
-    iota(T.ic[:], [[1, C]], 0, 0, ["ic"], True)
+    dma("A", T.ut[:], T.u[:], "d0", w=["ut"])
+    for k, (lo, hi) in enumerate(CH):
+        dma("S", T.xt[:, 4 * lo:4 * hi], T.x[:, 4 * lo:4 * hi], "d%d" % (1 + k), w=["xt_%d" % k])
+    for G in range(8):
+        s = 20 * (G & 1) + 2 * (G >> 1)
+        dma("S", T.cdl[16 * G:16 * G + 16, 0:454], T.cd[:, s:s + 454], "d5", w=["cdl%d" % G])
+    writer["cdl"] = ("d5", count["d5"])
+    dma("S", T.wq[:].bitcast(dt.uint8), T.wc[:], "d6", w=["wq"])
+    dma("S", T.wsc[:], T.ws[:], "d6", w=["wsc"])
+    writer["wq"] = writer["wsc"]
+    dma("S", T.vt[:], T.v[:], "d7", w=["vt"])
 
     def bf(i):
         return T.bf[:, i:i + 1]
@@ -200,322 +202,395 @@ def rank_program(g, core, T, topo):
         return T.fo[:, 32 * i:32 * i + 1]
 
     ms(T.warm[:], 0.0, ["warm"])
+    ms(T.ft5[:], 0.0, ["z5"])
+    iota(T.ip[:], [[0, 2]], 0, 1, ["ip"])
+    iota(T.li[:, 0:8], [[16, 8]], 0, 0, ["li_u"])
+    iota(T.i16[:], [[0, CUT // 16], [1, 16]], 0, 0, ["i16"], True)
+    op("G", lambda: g.affine_select(T.et[:], T.ft5[:, 0:1032], [[-1, 2], [1, 516]], A.not_equal, 1.0, -2, -4), r=["z5"], w=["et"])
+    iota(T.dgi[:, 0:256], [[1, 8], [0, 32]], 0, 0, ["dgi0"], True)
+    iota(T.dgi[:, 256:512], [[0, 8], [1, 8], [0, 4]], 0, 0, ["dgi1"], True)
+    iota(T.cmi[:], [[0, 8], [1, 8], [0, 8]], 0, 0, ["cmi"], True)
+    iota(T.tb[:], [[0, 3], [-1, 8], [1, 8]], 0, 0, ["tb"], True)
+    iota(T.ic[:], [[1, C]], 0, 0, ["ic"], True)
+    iota(T.fi[:, 0:16], [[0, 8], [8, 2]], 0, 0, ["fi0"], True)
+    iota(T.fi[:, 16:32], [[0, 8], [-4, 2]], 8, 0, ["fi7"], True)
+    for i, pat in enumerate(([[0, 8], [1, 2], [0, 2]], [[0, 4], [1, 2], [0, 4]], [[0, 2], [4, 2], [0, 8]],
+                             [[0, 4], [1, 8]], [[0, 4], [8, 8]], [[0, 2], [2, 2], [0, 8]])):
+        iota(T.fi[:, 32 * i + 32:32 * i + 64], pat, 0, 0, ["fi%d" % (i + 1)], True)
+    iota(T.li[:, 8:20], [[-8, 3], [0, 4]], 16, 0, ["li_w0", "li_w1"])
+    for name, pats in (("v", (([[0, 2], [64, 2], [0, 2]], 7), ([[0, 4]], 7))),
+                       ("uu", (([[1, 2], [-8, 2], [4, 2]], 40), ([[1, 2], [4, 2]], 24))),
+                       ("pc", (([[1, 2], [64, 2], [4, 2]], 0), ([[1, 2], [4, 2]], 0)))):
+        for k, (pat, base) in enumerate(pats):
+            c0 = LISTS[name] + 8 * k
+            iota(T.li[:, c0:c0 + 8 - 4 * k], pat, base, 0, ["li_%s%d" % (name, k)])
+
+    act(T.warm[:, 1:2], T.warm[:, 0:1], AF.Exp, ["warm"], ["warm1"])
+    ts(T.bi[:, 0:1], T.ip[:, 0:1], 15, None, A.bitwise_and, None, ["ip"], ["bi0"])
+    ts(T.bi[:, 1:2], T.ip[:, 0:1], 4, None, A.arith_shift_right, None, ["ip"], ["bi1"])
+    ts(T.bi[:, 2:3], T.ip[:, 0:1], 5, 1, A.arith_shift_right, A.bitwise_and, ["ip"], ["bi2"])
+    ts(T.bi[:, 3:4], T.ip[:, 0:1], 6, None, A.arith_shift_right, None, ["ip"], ["bi3"])
+    cp(T.lu[:, 0:8], T.li[:, 0:8], ["li_u"], ["lu_u"])
     ms(T.keep[:], 1.0, ["keep"])
     ms(T.rmin[:], -2.0 ** 30, ["rmin"])
-    act(T.warm[:, 1:2], T.warm[:, 0:1], AF.Exp, ["warm"], ["warm1"])
-    for i, m in enumerate((15, 32, 64, 7)):
-        ts(T.bi[:, i:i + 1], T.ip[:, 0:1], m, None, A.bitwise_and, None, ["ip"], ["bi%d" % i])
-    ts(T.bi[:, 4:5], T.ip[:, 0:1], 4, None, A.arith_shift_right, None, ["ip"], ["bi4"])
-    cp(T.lu[:, 0:8], T.li[:, 0:8], ["li_u"], ["lu_u"])
-    ms(T.keep[:, 0:C:8], 0.0, ["keep"])
-    ms(T.rmin[:, 0:160:8], 2.0 ** 30, ["rmin"])
-    cp(T.bf[:, 0:5], T.bi[:, 0:5], ["bi%d" % i for i in range(5)], ["bf"])
-    zeros = {1: ["z12", "z13"], 5: ["z51", "z52", "z53"]}
-    ms(T.ft1[:, 2:4 * H:4], 0.0, ["z12"])
-    ms(T.ft1[:, 3:4 * H:4], 0.0, ["z13"])
-    ms(T.ft5[:, 4 * H + 1:4 * C:4], 0.0, ["z51"])
-    ms(T.ft5[:, 4 * H + 2:4 * C:4], 0.0, ["z52"])
-    ms(T.ft5[:, 3:4 * C:4], 0.0, ["z53"])
-    ms(T.ft4[:, 0:4 * H], 0.0, ["z4"])
-    ts(cf(0), bf(1), 5.0, bf(0), A.mult, A.add, ["bf"], ["cf0"])
-    ts(cf(1), bf(2), 1.25, None, A.mult, None, ["bf"], ["cf1"])
-    ts(cf(2), bf(3), 0.0625, None, A.mult, None, ["bf"], ["cf2"])
-    ts(cf(3), bf(0), -2.0 ** 90, None, A.mult, None, ["bf"], ["cf3"])
-    quant(T.fq4, T.fs4, T.ft4, 0, H, ["z4"], ["fq4_0"])
-    for b in range(4):
-        for e in range(4):
-            act(T.et[:, 512 * b + e:512 * b + 512:4], T.ident[:], AF.Identity, ["ident"], ["et%d%d" % (b, e)],
-                scale=1.0 if b == e else 0.0)
-    act(T.negm[:], T.i16[:], AF.Abs, ["i16", "cf3"], ["negm"], scale=2.0 ** 90, bias=cf(3))
+    cp(T.bf[:], T.bi[:], ["bi%d" % i for i in range(4)], ["bf"])
+    ms(T.dtl[:, 0:512], 0.0, ["dtl0"])
+    ts(cf(0), bf(0), -2.0 ** 90, None, A.mult, None, ["bf"], ["cf0"])
+    ms(T.dtl[:, 768:1024], 0.0, ["dtl2"])
+    ms(T.keep[:, 0:192:8], 0.0, ["keep"])
+    ms(T.rmin[:, 0:128:8], 2.0 ** 30, ["rmin"])
     act(T.rst[:], T.i16[:], AF.Identity, ["i16"], ["rst"], scale=2.0 ** 96, bias=-2.0 ** 95)
-    act(T.ijg[:], T.ij[:], AF.Identity, ["ij", "cf2"], ["ijg"], bias=cf(2))
-    ts(T.ct[:, 0:512], T.cmi[:], bf(4), 512.0, A.is_equal, A.mult, ["cmi", "bf"], ["ct0"])
-    ts(T.ct[:, 512:1024], T.cmi[:], bf(4), 256.0, A.is_equal, A.mult, ["cmi", "bf"], ["ct1"])
+    act(T.negm[:], T.i16[:], AF.Abs, ["i16", "cf0"], ["negm"], scale=2.0 ** 90, bias=cf(0))
     quant(T.uq, T.us, T.ut, 0, 128, ["ut"], ["uq"])
-    quant(T.tq0, T.ts0, T.xt, 0, C, ["xt"], ["tq0_0", "tq0_1"])
-    cp(T.urq[:].bitcast(dt.uint32), T.uq[:].bitcast(dt.uint32).indirect(lst("u")), ["uq", "lu_u"], ["urq"])
-    cp(T.urs[:], T.us[:].indirect(lst("u")), ["uq", "lu_u"], ["urs"])
-    quant(T.cq, T.cs, T.ct, 0, 256, ["ct0", "ct1"], ["cq"])
+    cp(T.urq[:].bitcast(dt.uint32), T.uq[:].bitcast(dt.uint32).indirect(T.lu[:, 0:8]), ["uq", "lu_u"], ["urq"])
+    cp(T.urs[:], T.us[:].indirect(T.lu[:, 0:8]), ["uq", "lu_u"], ["urs"], q="A")
 
-    def late_constants():
-        quant(T.eq, T.es, T.et, 0, 512, ["et%d%d" % (b, e) for b in range(4) for e in range(4)], ["eq"])
-        turn(T.fo[:], T.fi[:], ["fi%d" % i for i in range(6)], ["fo"])
+    count_tiles = [
+        lambda: (ts(T.dgi[:], T.dgi[:], bf(1), 8.0, A.is_equal, A.mult, ["dgi0", "dgi1", "bf"], ["dgi0", "dgi1"]),
+                 ts(T.ct[:], T.cmi[:], bf(1), 2.0 ** -10, A.is_equal, A.mult, ["cmi", "bf"], ["ct"])),
+        lambda: (tt(T.dtl[:, 512:768], T.dgi[:, 0:256], T.dgi[:, 256:512], A.subtract, ["dgi0"], ["dtl1"]),
+                 ts(T.ct[:, 0:512:4], T.ct[:, 0:512:4], 2.0, None, A.mult, None, ["ct"], ["ct"])),
+        lambda: ts(T.dtl[:, 512:768:4], T.dtl[:, 512:768:4], 2.0, None, A.mult, None, ["dtl1"], ["dtl1"]),
+        lambda: (quant(T.cq, T.cs, T.ct, 0, 128, ["ct"], ["cq"]),
+                 quant(T.dq, T.ds, T.dtl, 0, 256, ["dtl0", "dtl1", "dtl2"], ["dq"])),
+    ]
 
-    def lists(names):
-        for name, c1, c2 in (("own", cf(0), cf(1)), ("cmp", fo(0), None), ("bad", fo(2), None), ("sel", fo(1), fo(3)),
-                             ("w", fo(4), None), ("v", fo(5), None), ("uu", fo(1), None)):
-            if name in names:
-                c0, n = LISTS[name]
-                ts(T.lu[:, c0:c0 + n], T.li[:, c0:c0 + n], c1, c2, A.add, None if c2 is None else A.add,
-                   ["li_" + name, "fo", "cf0", "cf1"], ["lu_" + name])
+    def unpack_tiles():
+        for b in range(4):
+            quant(T.eq, T.es, T.et, 128 * b, 128 * b + 128, ["et"], ["eq%d" % b], at=516 * (b % 2) + 2 - b // 2 * 2)
+
+    def column_terms():
+        n1 = len(ALATE)
+        n0 = len(AEARLY) + sum(1 for m in ALATE if m not in AEARLY + VEARLY)
+        for k, (lo, hi) in enumerate(CH):
+            act(T.ij[:, lo:hi], T.ic[:, lo:hi], AF.Identity, ["ic"], ["ij%d" % k], scale=2.0 ** -18,
+                bias=(8 * (n0, n1)[k] - 1) * 2.0 ** -9)
 
     def candidates():
-        for sl in range(5):
-            for g2 in range(2):
-                cp(T.cdu[:, 2 * sl + g2:120:10], T.cdl[:, sl:sl + 441:40], ["cdl"], ["cdu%d" % (2 * sl + g2)])
+        for s in range(3):
+            for h in range(2):
+                c = SLOT[s] // 16 + h
+                cp(T.cdu[:, 24 * s + h:24 * s + 24:2], T.cdl[:, c:c + 441:40], ["cdl"], ["cdu%d" % (2 * s + h)])
 
-    cdu_keys = ["cdu%d" % i for i in range(10)]
+    def lists():
+        for name, c1, c2 in (("w", fo(4), None), ("v", fo(5), None), ("uu", fo(6), None), ("pc", fo(5), fo(6))):
+            c0 = LISTS[name]
+            ts(T.lu[:, c0:c0 + 12], T.li[:, c0:c0 + 12], c1, c2, A.add, None if c2 is None else A.add,
+               ["li_%s0" % name, "li_%s1" % name, "fo"], ["lu_" + name])
+
+    final_lists = [
+        lambda: turn(T.fo[:], T.fi[:], ["fi%d" % i for i in range(8)], ["fo"]),
+        lambda: (ts(cf(1), fo(1), bf(2), 24.0, A.not_equal, A.mult, ["fo", "bf"], ["cf1"]),
+                 ts(cf(2), fo(2), bf(3), 12.0, A.not_equal, A.mult, ["fo", "bf"], ["cf2"]),
+                 ts(cf(3), bf(3), 2.0, bf(2), A.mult, A.add, ["bf"], ["cf3"]), lists()),
+        lambda: (ts(cf(4), cf(1), cf(2), fo(0), A.add, A.add, ["cf1", "cf2", "fo"], ["cf4"]),
+                 ts(cf(5), cf(3), fo(3), None, A.add, None, ["cf3", "fo"], ["cf5"])),
+        lambda: (ts(T.lu[:, 56:57], cf(4), 2.0, cf(5), A.mult, A.add, ["cf4", "cf5"], ["lu_f0"]),
+                 ts(T.lu[:, 58:59], cf(4), cf(3), None, A.add, None, ["cf4", "cf3"], ["lu_f1"])),
+    ]
+
+    cdu_keys = ["cdu%d" % i for i in range(6)]
+    eq_keys = ["eq%d" % i for i in range(4)]
     LN2 = math.log(2.0)
-    MAGIC = 1.5 * 2.0 ** 41
+    WHOLE = 1.5 * 2.0 ** 23
 
-    def scores(t, h):
-        for bank in (SV[h], SA[h]):
-            mm(bank, T.urq, T.urs, 0, T["tq%d" % t], T["ts%d" % t], H * h, H * h + H, True, True,
-               ["urq", "urs", "tq%d_%d" % (t, h)])
+    def own_part(k, t):
+        lo, hi = CH[k]
+        for i in range(4 if t else 0):
+            if XN[k][i] == "A":
+                mm(UB[i], T.eq, T.es, 128 * i, T["tq%d" % (t - 1)], T["ts%d" % (t - 1)], lo, hi, True, False,
+                   eq_keys + ["tq%d_%d" % (t - 1, k)])
 
-    def own_scores(h):
-        lo, hi, bk = H * h, H * h + H, "pb%d" % SV[h]
-        tt(T.pm[:, lo:hi], T[bk][:, 0:H], T.negm[:, lo:hi], A.subtract, ["negm"], ["pm%d" % h], x=[bk])
+    def summed(k, t):
+        if t == 0:
+            return
+        lo, hi = CH[k]
+        lq, ls = T["lq%d" % (t - 1)], T["ls%d" % (t - 1)]
+        arrives("lq_%d" % k, "ha%d" % (2 * (t - 1) + k), 2 * NENG)
+        for i in range(4):
+            mm(UB[i], T.eq, T.es, 128 * i, lq, ls, lo, hi, XN[k][i] == "V", True, eq_keys + ["lq_%d" % k])
 
-    def own_scan(h):
-        lo, hi = H * h, H * h + H
-        scan(T.th[:, lo:hi], T.rst[:, lo:hi], T.pm[:, lo:hi], A.min, A.max, ["rst", "pm%d" % h], ["th%d" % h])
+    def taken(k, t):
+        lo, hi = CH[k]
+        for i in range(4 if t else 0):
+            bk = "pb%d" % UB[i]
+            out, w = T.xn[:, 4 * lo + i:4 * hi:4], ["xn%d_%d" % (i, k)]
+            if XN[k][i] == "V":
+                tt(out, T[bk][:, 0:hi - lo], T.dtw[:, C * i + lo:C * i + hi], A.add, ["dtw%d" % i], w, x=[bk])
+            else:
+                cp(out, T[bk][:, 0:hi - lo], [], w, x=[bk], q="A")
 
-    def ties(h):
-        lo, bk = H * h, "pb%d" % SV[h]
-        tt(T.ft0[:, 4 * lo:4 * lo + 4 * H:4], T[bk][:, 0:H], T.th[:, lo:lo + H], A.is_equal, ["th%d" % h],
-           ["f0_0_%dl" % h], x=[bk])
+    def packed(k, t):
+        lo, hi = CH[k]
+        src, r = (T.xn, ["xn%d_%d" % (i, k) for i in range(4)]) if t else (T.xt, ["xt_%d" % k])
+        quant(T["tq%d" % t], T["ts%d" % t], src, lo, hi, r, ["tq%d_%d" % (t, k)])
 
-    def cut(m, h):
-        return min(max(16 * m + 16 - H * h, 0), H)
+    def scores(t, k, bank):
+        hi = CH[k][1]
+        mm(bank, T.urq, T.urs, 0, T["tq%d" % t], T["ts%d" % t], 0, hi, True, True, ["urq", "urs"] + keys("tq%d" % t, 0, hi))
 
-    def vrow(m, h, f, e):
-        ft, c, lo, sc, bk = T["ft%d" % f], cut(m, h), H * h, T.th[:, 16 * m + 15:16 * m + 16], "pb%d" % SV[h]
-        k, o = (None, None) if f < 3 else (2.0, A.mult)
-        if c > 0:
-            ts(ft[:, 4 * lo + e:4 * (lo + c):4], T[bk][:, 0:c], sc, k, A.is_lt, o, ["th%d" % (m // 10)],
-               ["f%d_%d_%dl" % (f, e, h)], x=[bk])
-        if c < H:
-            ts(ft[:, 4 * (lo + c) + e:4 * (lo + H):4], T[bk][:, c:H], sc, k, A.is_le, o, ["th%d" % (m // 10)],
-               ["f%d_%d_%dr" % (f, e, h)], x=[bk])
+    def parts(m, k):
+        a, c, hi = (CUT if k and m in VEARLY + AEARLY else 0), 16 * m + 16, CH[k][1]
+        return [(s, x, y) for s, x, y in (("l", a, min(c, hi)), ("r", max(a, c), hi)) if x < y]
 
-    def arows(rows, base):
+    def thk(m):
+        return keys("th", 16 * m, 16 * m + 16)
+
+    def vrow(m, k):
+        f, e = divmod(m, 4)
+        k2, o = (None, None) if e == 0 else (2.0, A.mult)
+        bk = "pb%d" % VB[k]
+        for s, a, b in parts(m, k):
+            ts(T["ft%d" % f][:, 4 * a + e:4 * b:4], T[bk][:, a:b], T.th[:, 16 * m + 15:16 * m + 16], k2,
+               A.is_lt if s == "l" else A.is_le, o, thk(m), keys("f%d%d%s" % (f, e, s), a, b), x=[bk])
+
+    def arows(rows):
         def one(i):
-            m, h, f, e = rows[i]
-            k, bk = base + i, "pb%d" % SA[h]
-            act(T.sg[:, H * k:H * k + H], T[bk][:, 0:H], AF.Sign, ["th%d" % (m // 10)], ["sg%d" % k], x=[bk],
+            m, k = rows[i]
+            a, hi, j, bk = parts(m, k)[0][1], CH[k][1], i % 4, "pb%d" % AB[k]
+            act(T.sg[:, C * j + a:C * j + hi], T[bk][:, a:hi], AF.Sign, thk(m), ["sg%d" % j], x=[bk],
                 bias=T.th[:, 16 * m + 15:16 * m + 16], scale=-1.0)
 
         def two(i):
-            m, h, f, e = rows[i]
-            k = base + i
-            ft, c, lo = T["ft%d" % f], cut(m, h), H * h
-            if c > 0:
-                act(ft[:, 4 * lo + e:4 * (lo + c):4], T.sg[:, H * k:H * k + c], AF.Sign, ["sg%d" % k],
-                    ["f%d_%d_%dl" % (f, e, h)], bias=-0.5)
-            if c < H:
-                act(ft[:, 4 * (lo + c) + e:4 * (lo + H):4], T.sg[:, H * k + c:H * k + H], AF.Sign, ["sg%d" % k],
-                    ["f%d_%d_%dr" % (f, e, h)], bias=0.5)
-        one(0)
-        for i in range(len(rows)):
-            if i + 1 < len(rows):
-                one(i + 1)
-            two(i)
+            m, k = rows[i]
+            f, e = divmod(m, 4)
+            for s, a, b in parts(m, k):
+                act(T["ft%d" % f][:, 4 * a + e:4 * b:4], T.sg[:, C * (i % 4) + a:C * (i % 4) + b], AF.Sign, ["sg%d" % (i % 4)],
+                    keys("f%d%d%s" % (f, e, s), a, b), bias=-0.5 if s == "l" else 0.5)
+        for i in range(len(rows) + 2):
+            if i < len(rows):
+                one(i)
+            if i >= 2:
+                two(i - 2)
 
-    def qflags(f, halves):
-        keys = ["f%d_%d_%d%s" % (f, e, h, s) for e in range(4) for h in halves for s in "lr"] + zeros.get(f, [])
-        quant(T["fq%d" % f], T["fs%d" % f], T["ft%d" % f], H * halves[0], H * halves[-1] + H, keys,
-              ["fq%d_%d" % (f, h) for h in halves])
+    def own_scores(k):
+        lo, hi = CH[k]
+        bk = "pb%d" % VB[k]
+        tt(T.pm[:, lo:hi], T[bk][:, lo:hi], T.negm[:, 0:hi - lo], A.subtract, ["negm"], ["pm%d" % k], x=[bk])
 
-    def tally(f, n=C):
-        mm(CNT, T.cq, T.cs, 0 if f < 3 else 1, T["fq%d" % f], T["fs%d" % f], 0, n, f == 0, f == 6,
-           ["cq", "fq%d_0" % f, "fq%d_1" % f])
+    def held(k):
+        lo, hi = CH[k]
+        scan(T.th[:, lo:hi], T.rst[:, 0:hi - lo], T.pm[:, lo:hi], A.min, A.max, ["rst", "pm%d" % k], ["th_%d" % k])
 
-    def early(t):
-        scores(t, 0)
+    def ties(k):
+        lo, hi = CH[k]
+        bk = "pb%d" % VB[k]
+        tt(T.ft5[:, 4 * lo:4 * hi:4], T[bk][:, lo:hi], T.th[:, lo:hi], A.is_equal, ["th_%d" % k, "et"], ["f50l_%d" % k], x=[bk])
+
+    def places(t):
+        done = []
+
+        def finish(f):
+            fq, fs, key = T["fq%d" % f], T["fs%d" % f], ["fq%d" % f]
+            quant(fq, fs, T["ft%d" % f], 0, C,
+                  ["z5"] + [x for e in range(4) for s in "lr" for x in keys("f%d%d%s" % (f, e, s), 0, C)], key)
+            done.append(f)
+            for s in range(3):
+                mm(DB, fq, fs, SLOT[s], T.dq, T.ds, 64 * s, 192 + 64 * (s // 2), len(done) == 1 and s == 0,
+                   len(done) == 6 and s == 2, ["dq"] + key)
+            for x in {5: [], 6: done[4:]}.get(len(done), [f]):
+                mm(CNT, T.cq, T.cs, 0, T["fq%d" % x], T["fs%d" % x], 0, C, len(done) == 1, x == done[-1] and len(done) == 6,
+                   ["cq", "fq%d" % x])
+
+        fill = list(count_tiles) if t == 0 else []
+
+        def filler():
+            if fill:
+                fill.pop(0)()
+        own_part(0, t)
+        summed(0, t)
+        taken(0, t)
+        own_part(1, t)
+        if not LATE1:
+            summed(1, t)
+        packed(0, t)
+        scores(t, 0, VB[0])
+        scores(t, 0, AB[0])
+        if not LATE1:
+            taken(1, t)
+            if t:
+                packed(1, t)
         own_scores(0)
-        own_scan(0)
-        arows([(9, 0, 3, 0), (8, 0, 3, 1), (7, 0, 3, 2), (6, 0, 3, 3), (0, 0, 5, 1)], 0)
-        ties(0)
-        for i, m in enumerate((1, 2, 3, 4, 5)):
-            vrow(m, 0, (i + 1) // 4, (i + 1) % 4)
-            if i == 3:
-                qflags(0, [0])
-        qflags(1, [0])
+        if not LATE1 and not t:
+            packed(1, t)
+        if LATE1:
+            summed(1, t)
+            taken(1, t)
+        held(0)
+        if LATE1:
+            packed(1, t)
+            ties(0)
+        scores(t, 1, VB[1])
+        scores(t, 1, AB[1])
+        if not LATE1:
+            ties(0)
+        early = [(m, 0) for m in AEARLY]
+        first = [(m, 1) for m in ALATE if 16 * m < CUT]
+        arows(early + first[:-2])
+        for m in VEARLY[:1]:
+            vrow(m, 0)
+        own_scores(1)
+        for m in VEARLY[1:2]:
+            vrow(m, 0)
+        held(1)
+        arows(first[-2:] + [(m, 1) for m in ALATE if 16 * m >= CUT])
+        for m in VEARLY[2:]:
+            vrow(m, 0)
+        ties(1)
 
-    early(0)
-    late_constants()
+        def width(m, k):
+            return CH[k][1] - parts(m, k)[0][1]
+        last = {f: max([i for i, m in enumerate(ALATE) if m // 4 == f] + [-1]) for f in range(6)}
+        ends = {f: 2 * sum(width(m, 1) for m in ALATE[:last[f] + 1]) for f in range(6)}
+        order = sorted(range(5), key=lambda f: (last[f], -f))
+        rows = [m for f in order for m in range(4 * f, 4 * f + 4) if m not in ALATE]
+        due, passed = [5] + order, 0
+        for i, m in enumerate(rows):
+            vrow(m, 1)
+            filler()
+            passed += width(m, 1)
+            for f in [f for f in due if not fill and ends[f] + LAG <= passed and not any(x // 4 == f for x in rows[i:])]:
+                finish(f)
+                due.remove(f)
+                passed += C
+        for f in due:
+            finish(f)
 
     for t in range(R):
         donor = T.cores[(rank + 1 + t) % N]
         child = T.cores[(rank - 1 - t) % N]
-        tq, tsc, tk = T["tq%d" % t], T["ts%d" % t], ["tq%d_0" % t, "tq%d_1" % t]
-
-        def unpack(b):
-            mm(DTB[b], T.eq, T.es, b, tq, tsc, 0, C, True, True, ["eq"] + tk)
+        tq, tsc, tk = T["tq%d" % t], T["ts%d" % t], keys("tq%d" % t, 0, C)
+        places(t)
+        if t == 0:
+            column_terms()
+            unpack_tiles()
+        for b in range(4):
+            mm(UB[b], T.eq, T.es, 128 * b, tq, tsc, 0, C, True, True, eq_keys + tk)
 
         def window(b):
-            bk = "pb%d" % DTB[b]
+            bk = "pb%d" % UB[b]
             act(T.dtw[:, C * b:C * b + C], T[bk][:, 0:C], AF.Copy, [], ["dtw%d" % b], x=[bk])
 
-        scores(t, 1)
-        for b in range(3):
-            unpack(b)
-        qflags(3, [0])
-        own_scores(1)
-        vrow(9, 1, 2, 3)
-        own_scan(1)
-        arows([(0, 1, 3, 0), (1, 1, 3, 1), (2, 1, 3, 2), (3, 1, 3, 3), (4, 1, 5, 0), (14, 0, 5, 0), (15, 0, 5, 2),
-               (5, 1, 4, 0), (6, 1, 4, 1), (7, 1, 4, 2), (8, 1, 4, 3),
-               (16, 0, 6, 0), (17, 0, 6, 1), (18, 0, 6, 2)], 5)
-        if t == 0:
-            lists(("own", "cmp"))
-        ties(1)
-        for m in range(10, 14):
-            vrow(m, 1, (m - 9) // 4, (m - 9) % 4)
-        qflags(0, [1])
-        tally(0)
-        for m in range(14, 18):
-            vrow(m, 1, (m - 9) // 4, (m - 9) % 4)
-        qflags(1, [1])
-        tally(1)
-        qflags(3, [1])
-        tally(3)
-        vrow(18, 1, 2, 1)
-        vrow(19, 1, 2, 2)
-        for m in range(10, 14):
-            vrow(m, 0, 2, m - 10)
-        qflags(5, [0, 1])
-        tally(5)
-        vrow(19, 0, 6, 3)
-        qflags(2, [0, 1])
-        tally(2)
-        qflags(4, [1])
-        tally(4)
-        qflags(6, [0])
-        tally(6, H)
-        unpack(3)
+        wo, wl = T["wo%d" % t], T["wl%d" % t]
         if t == 0:
             candidates()
-        window(0)
-        window(1)
+        tt(T.fl[:], T["pb%d" % DB][:, 0:192], T.tb[:], A.is_gt, ["tb"], ["fl"], x=["pb%d" % DB])
+        tt(T.pcw[:], T["pb%d" % CNT][:, 0:C], T.ij[:], A.add, ["ij0", "ij1"], ["pcw"], x=["pb%d" % CNT])
+        scan(T.ps[:], T.keep[:], T.fl[:], A.mult, A.add, ["keep", "fl"], ["ps"])
 
-        tt(T.pcw[:], T["pb%d" % CNT][:, 0:C], T.ijg[:], A.add, ["ijg"], ["pcw"], x=["pb%d" % CNT])
-        cp(T.gk[:], T.pcw[:].indirect(lst("own")), ["pcw", "lu_own"], ["gk"])
-        for h in range(2):
-            act(T.gc1[:, C * h:C * h + C], T.pcw[:].indirect(T.cdu[:, 40 * t + 20 * h:40 * t + 20 * h + 20]), AF.Copy,
-                ["pcw"] + cdu_keys, ["gc%d" % h])
-        turn(T.tk[:, 0:160], T.gk[:], ["gk"], ["tk"])
-        turn(T.tk[:, 160:C], T.gk[:], ["gk"], ["tk2"])
-        for h in range(2):
-            tt(T.fl[:, 160 * h:160 * h + 160], T.tk[:, 160:C].indirect(lst("cmp", 10 * h, 10 * h + 10)), T.tk[:, 0:160],
-               A.is_gt, ["tk", "tk2", "lu_cmp"], ["fl%d" % h])
-        scan(T.ps[:], T.keep[:], T.fl[:], A.mult, A.add, ["keep", "fl0", "fl1"], ["ps"])
-        wo, wl = T["wo%d" % t], T["wl%d" % t]
-        act(wo[:, 0:40], T.ps[:, 7:C:8], AF.Exp, ["ps"], ["wo0"], scale=-LN2, bias=7 * LN2)
-        cp(wo[:, 40:80], T.ps[:, 7:C:8], ["ps"], ["wo1"])
+        def gather(s, q):
+            cp(T.gc1[:, 128 * s:128 * s + 128], T.pcw[:].indirect(T.cdu[:, 24 * s + 8 * t:24 * s + 8 * t + 8]),
+               ["pcw"] + cdu_keys, ["gc%d" % s], q=q)
+        gather(0, "V")
+        act(wo[:, 0:24], T.ps[:, 7:192:8], AF.Exp, ["ps"], ["wo0"], scale=-LN2, bias=7 * LN2)
+        cp(wo[:, 24:48], T.ps[:, 7:192:8], ["ps"], ["wo1"], q="A")
         send(donor, wl[:], wo[:], "wa%d" % t, ["wo0", "wo1"])
-
+        gather(1, "A")
+        gather(2, "A")
+        for s in range(3):
+            turn(T.tg[:, 128 * s:128 * s + 128], T.gc1[:, 128 * s:128 * s + 128], ["gc%d" % s], ["tg%d" % s])
         if t == 0:
-            lists(("bad", "sel", "w", "v", "uu"))
-        turn(T.tg[:, 0:C], T.gc1[:, 0:C], ["gc0"], ["tg0"])
-        turn(T.tg[:, C:2 * C], T.gc1[:, C:2 * C], ["gc1"], ["tg1"])
-        window(2)
-        tgk = ["tg0", "tg1"]
-        thr = 512.0 * TH
-        act(T.sb[:, 0:160], T.tg[:].indirect(lst("sel")), AF.Sign, tgk + ["lu_sel"], ["sb"], bias=0.25 - thr)
-        act(T.sb[:, 160:C], T.sb[:, 0:160], AF.Identity, ["sb"], ["tt"], scale=-2.0 ** 17, bias=-2.0 ** 17)
-        ts(T.bad[:], T.tg[:].indirect(lst("bad")), thr, None, A.is_ge, None, tgk + ["lu_bad"], ["bad"])
-
-        arrives("wl", "wa%d" % t, NENG)
-        act(T.ub[:], wl[:].indirect(lst("uu")), AF.Exp, ["wl", "lu_uu"], ["ub"], scale=LN2,
-            bias=10 * LN2 + math.log(1.0 + 2.0 ** -9))
-        window(3)
-        tt(T.pc2[:], T.tg[:].indirect(lst("sel")), T.sb[:, 160:C], A.add, tgk + ["lu_sel", "tt"], ["pc2"])
-        tt(T.dd[:], wl[:].indirect(lst("w")), T.bad[:], A.mult, ["wl", "lu_w", "bad"], ["dd"])
-        scan(T.vv[:], T.keep[:], T.dd[:], A.mult, A.add, ["keep", "dd"], ["vv"])
-        yy, zz, ky = T.yy[:, 0:160], T.yy[:, 160:320], T.yy[:, 320:480]
-        tt(yy, T.vv[:].indirect(lst("v")), T.ub[:], A.mult, ["vv", "lu_v", "ub"], ["yy"])
-        ts(zz, yy, MAGIC, -(MAGIC + 2.0 ** 24), A.add, A.add, ["yy"], ["zz"])
-        tt(ky, zz, T.pc2[:], A.add, ["zz", "pc2"], ["ky"])
-        scan(T.mn[:], T.rmin[:], ky, A.max, A.min, ["rmin", "ky"], ["mn"])
-        for a1 in range(2):
-            for b1 in range(2):
-                cp(T.e1[64 * b1:64 * b1 + 64, 10 * a1:10 * a1 + 10], T.mn[64 * a1:64 * a1 + 64, 80 * b1 + 7:80 * b1 + 80:8],
-                   ["mn"], ["e1_%d%d" % (a1, b1)])
-        ts(T.e1[:, 20:40], T.e1[:, 0:20], 511, None, A.bitwise_and, None, ["e1_00", "e1_01", "e1_10", "e1_11"], ["e2"])
-        eok = [["eo%d%d" % (h, i) for i in range(4)] for h in range(2)]
-
-        def leaders(a0):
-            for b1 in range(2):
-                for b0 in range(2):
-                    src, dst = 64 * b1 + 32 * a0, 64 * b1 + 32 * b0
-                    cp(T.eo[dst:dst + 32, 10 * a0:10 * a0 + 10], T.e1[src:src + 32, 20 + b0:40:2], ["e2"],
-                       [eok[a0][2 * b1 + b0]])
-
-        zq, zs, hq, hs, lq, ls = (T["%s%d" % (n, t)] for n in ("zq", "zs", "hq", "hs", "lq", "ls"))
-        banks = ((3, 4, 5, 6), (0, 1, 2, 7))
-
-        def part(h, b, q):
-            out, win = T.zt[:, 4 * H * h + b:4 * H * (h + 1):4], T.dtw[:, C * b:C * b + C].indirect(T.eo[:, 10 * h:10 * h + 10])
-            if q == "V":
-                cp(out, win, ["dtw%d" % b] + eok[h], ["zt%d%d" % (b, h)])
-            else:
-                act(out, win, AF.Copy, ["dtw%d" % b] + eok[h], ["zt%d%d" % (b, h)])
-
-        def layer(h):
-            quant(zq, zs, T.zt, H * h, H * h + H, ["zt%d%d" % (b, h) for b in range(4)], ["zq%d" % h])
-            for b in range(4):
-                mm(banks[h][b], T.wq, T.wsc, b, zq, zs, H * h, H * h + H, True, True, ["wq", "zq%d" % h])
-
-        def relu(h, b, q):
-            bk, out = "pb%d" % banks[h][b], T.ht[:, 4 * H * h + b:4 * H * (h + 1):4]
-            if q == "V":
-                ts(out, T[bk][:, 0:H], 0.0, 0.015625, A.max, A.mult, [], ["ht%d%d" % (b, h)], x=[bk])
-            else:
-                act(out, T[bk][:, 0:H], AF.Relu, [], ["ht%d%d" % (b, h)], x=[bk], scale=0.015625)
-
-        def ship(h):
-            lo, hi = H * h, H * h + H
-            quant(hq, hs, T.ht, lo, hi, ["ht%d%d" % (b, h) for b in range(4)], ["hq%d" % h])
-            send(child, lq[:, lo:hi].bitcast(dt.uint8), hq[:, lo:hi].bitcast(dt.uint8), "ha%d" % (2 * t + h), ["hq%d" % h])
-            send(child, ls[:, lo:hi], hs[:, lo:hi], "ha%d" % (2 * t + h), ["hq%d" % h])
-        leaders(0)
-        for b in range(4):
-            part(0, b, "VA"[b % 2])
-        layer(0)
-        leaders(1)
-        for b in range(4):
-            part(1, b, "A")
-            relu(0, b, "V")
-        ship(0)
-        layer(1)
-        if t == R - 1:
-            ts(T.elb[:], T.ic[:].indirect(T.eo[:]), 0.0, None, A.add, None, ["ic"] + eok[0] + eok[1], ["elb"])
-            dma("S", T.el[:], T.elb[0:128:16, :], "d5", r=["elb"])
-        for b in range(4):
-            relu(1, b, "AV"[b % 2])
-        ship(1)
-        if t == 0:
+            weave(final_lists)
             quant(T.vq, T.vs, T.vt, 0, 128, ["vt"], ["vq"])
+        zq, zs, hq, hs, lq, ls = (T["%s%d" % (n, t)] for n in ("zq", "zs", "hq", "hs", "lq", "ls"))
+        arrives("wl", "wa%d" % t, NENG)
 
-        nq, ns = T["tq%d" % (t + 1)], T["ts%d" % (t + 1)]
-        for h in range(2):
-            lo, hi = H * h, H * h + H
-            for b in range(4):
-                mm(3 + b, T.eq, T.es, b, tq, tsc, lo, hi, True, False, ["eq"] + tk)
-            arrives("lq%d" % h, "ha%d" % (2 * t + h), 2 * NENG)
-            for b in range(4):
-                bk, out = "pb%d" % (3 + b), T.xn[:, 4 * lo + b:4 * hi:4]
-                mm(3 + b, T.eq, T.es, b, lq, ls, lo, hi, False, True, ["eq", "lq%d" % h])
-                if ("AVVV" if h == 1 and t + 1 < R else "AVAV")[b] == "V":
-                    cp(out, T[bk][:, 0:H], [], ["xn%d%d" % (b, h)], x=[bk])
-                else:
-                    act(out, T[bk][:, 0:H], AF.Copy, [], ["xn%d%d" % (b, h)], x=[bk])
-            quant(nq, ns, T.xn, lo, hi, ["xn%d%d" % (b, h) for b in range(4)], ["tq%d_%d" % (t + 1, h)])
-            if t + 1 < R:
-                if h == 0:
-                    early(t + 1)
-            else:
-                key = "tq%d_%d" % (R, h)
-                mm(h, T.vq, T.vs, 0, nq, ns, lo, hi, True, True, ["vq", key])
-                dma("S", T.oc[:, 4 * lo:4 * hi], nq[:, lo:hi].bitcast(dt.uint8), "d%d" % (6 + h), r=[key])
-                cp(T.yb[:, lo:hi], T["pb%d" % h][:, 0:H], [], ["yb%d" % h], x=["pb%d" % h])
-                if h == 1:
-                    for k in range(4):
-                        dma("A" if k % 2 else "S", T.osc[4 * k:4 * k + 4, :], ns[32 * k:32 * k + 4, :], "d10",
-                            r=["tq%d_0" % R, key])
-                dma("S" if h == 0 else "A", T.y[:, lo:hi], T.yb[:, lo:hi], "d%d" % (8 + h), r=["yb%d" % h])
+        def chain(k):
+            lo, hi = CH[k]
+            a, n = 128 * k, 128 - 64 * k
+            e, m0, st = 24 - 12 * k, 192 * k, 2 - k
+            tgk, tgv = ["tg0", "tg1"] if k == 0 else ["tg2"], T.tg[:, 2 * a:2 * (a + n):2]
+            yy, zz, ky = (T.yy[:, 192 * i + a:192 * i + a + n] for i in range(3))
+            ci, cj, banks = 48 * k, 96 * k, (UB if k else (SV, SA, DB, CNT))
+            ends = T.mn[:, m0 + 7:m0 + n + n // 2:8]
+
+            def s(name):
+                return "%s.%d" % (name, k)
+
+            def whole():
+                r = [s("mn"), s("mx")]
+                ts(T.ci[:, ci:ci + e], ends, 2.0 ** 18, None, A.mult, None, r, [s("ci")])
+                for h in range(2):
+                    ts(T.ci[64 * h:64 * h + 64, ci + e:ci + 2 * e], T.mn[64 - 64 * h:128 - 64 * h, m0 + 7:m0 + n + n // 2:8],
+                       2.0 ** 18, None, A.mult, None, r, [s("ci%d" % h)])
+
+            def columns():
+                r = [s("ci"), s("ci0"), s("ci1")]
+                ts(T.cj[:, cj:cj + 2 * e], T.ci[:, ci:ci + 2 * e], 511, None, A.bitwise_and, None, r, [s("cj")])
+                for b in range(4):
+                    ts(T.cj[32 * b:32 * b + 32, cj + 2 * e:cj + 4 * e], T.ci[32 * (b ^ 1):32 * (b ^ 1) + 32, ci:ci + 2 * e], 511, None,
+                       A.bitwise_and, None, r, [s("cj%d" % b)])
+
+            def mosaic():
+                for b in range(4):
+                    cp(T.zt[:, 4 * lo + b:4 * hi:4], T.dtw[:, C * b:C * b + C].indirect(T.eo[:, 16 * k:16 * k + (hi - lo) // 16]),
+                       ["dtw%d" % b, s("eo")], [s("zt%d" % b)], q=ZQ[k][b])
+
+            def layer():
+                quant(zq, zs, T.zt, lo, hi, [s("zt%d" % b) for b in range(4)], [s("zq")])
+                for b in range(4):
+                    mm(banks[b], T.wq, T.wsc, 128 * b, zq, zs, lo, hi, True, True, ["wq", s("zq")])
+
+            def relu():
+                for b in range(4):
+                    bk, out = "pb%d" % banks[b], T.ht[:, 4 * lo + b:4 * hi:4]
+                    if HQ[k][b] == "V":
+                        ts(out, T[bk][:, 0:hi - lo], 0.0, 0.015625, A.max, A.mult, [], [s("ht%d" % b)], x=[bk])
+                    else:
+                        act(out, T[bk][:, 0:hi - lo], AF.Relu, [], [s("ht%d" % b)], x=[bk], scale=0.015625)
+
+            def ship():
+                quant(hq, hs, T.ht, lo, hi, [s("ht%d" % b) for b in range(4)], [s("hq")])
+                send(child, lq[:, lo:hi].bitcast(dt.uint8), hq[:, lo:hi].bitcast(dt.uint8), "ha%d" % (2 * t + k), [s("hq")])
+                send(child, ls[:, lo:hi], hs[:, lo:hi], "ha%d" % (2 * t + k), [s("hq")])
+
+            return [
+                lambda: ts(T.bad[:, a:a + n], tgv, TH * 2.0 ** -9, None, A.is_ge, None, tgk, [s("bad")]),
+                lambda: (act(T.ub[:, a:a + n], wl[:].indirect(lst("uu", k)), AF.Exp, ["wl", "lu_uu"], [s("ub")], scale=LN2,
+                             bias=-8 * LN2 + math.log(1.0 + 2.0 ** -9)),
+                         tt(T.dd[:, a:a + n], wl[:].indirect(lst("w", k)), T.bad[:, a:a + n], A.mult, ["wl", "lu_w", s("bad")], [s("dd")])),
+                lambda: (scan(T.vv[:, a:a + n], T.keep[:, 0:n], T.dd[:, a:a + n], A.mult, A.add, ["keep", s("dd")], [s("vv")]),
+                         tt(T.pc2[:, a:a + n], tgv, T.bad[:, a:a + n], A.subtract, tgk + [s("bad")], [s("pc2")]),
+                         window(2 * k), window(2 * k + 1)),
+                lambda: tt(yy, T.vv[:, a:a + n].indirect(lst("v", k)), T.ub[:, a:a + n], A.mult, [s("vv"), "lu_v", s("ub")], [s("yy")]),
+                lambda: ts(zz, yy, WHOLE, -(WHOLE + 64.0), A.add, A.add, [s("yy")], [s("zz")]),
+                lambda: tt(ky, T.pc2[:, a:a + n].indirect(lst("pc", k)), zz, A.add, [s("zz"), s("pc2"), "lu_pc"], [s("ky")]),
+                lambda: scan(T.mn[:, m0:m0 + n], T.rmin[:, 0:n], ky, A.max, A.min, ["rmin", s("ky")], [s("mn")]),
+                lambda: turn(T.rb[:, 64 * k:64 * k + 64], T.mn[:, m0 + st - 1:m0 + n:st], [s("mn")], [s("rb")]),
+                lambda: turn(T.mn[:, m0 + n + st - 1:m0 + n + n // 2:st], T.rb[:, 64 * k + 16:64 * k + 48], [s("rb")], [s("mx")]),
+                whole, columns,
+                lambda: cp(T.eo[:, 16 * k:16 * k + 16], T.cj[:, cj:cj + 4 * e].indirect(T.lu[:, 56 + 2 * k:57 + 2 * k]),
+                           ["lu_f%d" % k, s("cj")] + [s("cj%d" % b) for b in range(4)], [s("eo")]),
+                mosaic, layer, relu, ship]
+
+        weave(chain(0), [None] * SKEW + chain(1))
+        if t == R - 1:
+            for k, (lo, hi) in enumerate(CH):
+                cp(T.elb[:, lo:hi], T.ic[:].indirect(T.eo[:, 16 * k:16 * k + (hi - lo) // 16]), ["ic", "eo.%d" % k], ["elb%d" % k], q="A")
+            dma("S", T.el[:], T.elb[0:128:16, :], "d8", r=["elb0", "elb1"])
+
+    nq, ns = T["tq%d" % R], T["ts%d" % R]
+
+    def last(k):
+        lo, hi = CH[k]
+        bk, key = "pb%d" % (SV + k), ["tq%d_%d" % (R, k)]
+
+        def store():
+            packed(k, R)
+            mm(SV + k, T.vq, T.vs, 0, nq, ns, lo, hi, True, True, ["vq"] + key)
+            dma("S", T.oc[:, 4 * lo:4 * hi], nq[:, lo:hi].bitcast(dt.uint8), "d%d" % (9 + k), r=key)
+            if k:
+                for i in range(4):
+                    dma("AS"[i % 2], T.osc[4 * i:4 * i + 4, :], ns[32 * i:32 * i + 4, :], "d13", r=keys("tq%d" % R, 0, C))
+        return [lambda: (own_part(k, R), summed(k, R), taken(k, R)), store,
+                lambda: (cp(T.yb[:, lo:hi], T[bk][:, 0:hi - lo], [], ["yb%d" % k], x=[bk]),
+                         dma("SA"[k], T.y[:, lo:hi], T.yb[:, lo:hi], "d%d" % (14 + k), r=["yb%d" % k]))]
+    weave(last(0), [None] + last(1))
 
     for sem in sorted(count):
         wait("G", (sem, count[sem]))
+
+
+SKEW = 0
+ZQ = ("VAVA", "VAVA")
+HQ = ("VAVA", "VAVA")

import math
from concourse.mybir import dt, AluOpType, ActivationFunctionType

C, TH, R, N = 320, 240, 3, 8
CUT = 192
CH = ((0, CUT), (CUT, C))
SLOT = (0, 128, CUT)
VEARLY = (0, 4, 8)
AEARLY = (1, 2, 3)
ALATE = (1, 2, 3, 5, 6, 7, 9, 10, 11, 13)
XN = ("AVAV", "AVAV")
LAG = 600
LATE1 = 0
F32, BF, I32, U16, Q4, U8 = "float32", "bfloat16", "int32", "uint16", "float8_e4m3fn_x4", "uint8"


def _s(n, d):
    return ("sbuf", [128, n], d)


SCRATCH = {
    "xt": _s(4 * C, BF), "ut": _s(512, BF), "vt": _s(512, BF), "cdl": _s(456, I32),
    "uq": _s(128, Q4), "us": _s(128, U8), "urq": _s(128, Q4), "urs": _s(128, U8), "vq": _s(128, Q4), "vs": _s(128, U8),
    "wq": _s(512, Q4), "wsc": _s(512, U8),
    "et": _s(1032, BF), "eq": _s(512, Q4), "es": _s(512, U8),
    "cmi": _s(512, BF), "ct": _s(512, BF), "cq": _s(128, Q4), "cs": _s(128, U8),
    "dgi": _s(512, BF), "dtl": _s(1024, BF), "dq": _s(256, Q4), "ds": _s(256, U8), "tb": _s(192, F32),
    "ip": _s(2, I32), "bi": _s(4, I32), "bf": _s(4, F32), "cf": _s(8, F32), "fi": _s(224, F32), "fo": _s(224, F32),
    "li": _s(56, I32), "lu": _s(60, U16), "cdu": _s(72, U16),
    "i16": _s(CUT, F32), "ij": _s(C, F32), "ic": _s(C, F32), "negm": _s(CUT, F32), "rst": _s(CUT, F32),
    "keep": _s(192, BF), "rmin": _s(128, F32), "warm": _s(2, F32),
    "pm": _s(C, F32), "th": _s(C, F32), "sg": _s(4 * C, BF), "fl": _s(192, BF), "ps": _s(192, BF),
    "pcw": _s(C, F32), "gc1": _s(384, F32), "tg": _s(384, F32), "bad": _s(192, BF), "pc2": _s(192, F32),
    "ub": _s(192, F32), "dd": _s(192, BF), "vv": _s(192, BF), "yy": _s(576, F32),
    "mn": _s(288, F32), "rb": _s(128, F32), "ci": _s(72, I32), "cj": _s(144, I32), "eo": _s(32, U16), "elb": _s(C, F32),
    "dtw": _s(4 * C, BF), "zt": _s(4 * C, BF), "ht": _s(4 * C, BF), "xn": _s(4 * C, BF), "yb": _s(C, F32),
}
for _i in range(6):
    SCRATCH["ft%d" % _i] = _s(4 * C, BF)
    SCRATCH["fq%d" % _i] = _s(C, Q4)
    SCRATCH["fs%d" % _i] = _s(C, U8)
for _i in range(R + 1):
    SCRATCH["tq%d" % _i] = _s(C, Q4)
    SCRATCH["ts%d" % _i] = _s(C, U8)
for _i in range(R):
    for _n in ("z", "h", "l"):
        SCRATCH["%sq%d" % (_n, _i)] = _s(C, Q4)
        SCRATCH["%ss%d" % (_n, _i)] = _s(C, U8)
    SCRATCH["wo%d" % _i] = _s(48, BF)
    SCRATCH["wl%d" % _i] = _s(48, BF)
for _i in range(8):
    SCRATCH["pb%d" % _i] = ("psum", [128, 512], F32)

SEMAPHORES = (["cV", "cA", "cP", "cG", "left"] + ["wa%d" % i for i in range(R)] + ["ha%d" % i for i in range(2 * R)]
              + ["d%d" % i for i in range(16)])

LISTS = {"w": 8, "v": 20, "uu": 32, "pc": 44}
UB, SV, SA, DB, CNT = (0, 1, 2, 3), 4, 5, 6, 7
VB, AB = (CNT, SV), (SA, UB[0])


def rank_program(g, core, T, topo):
    rank = T.rank_of(core)
    if rank is None:
        return
    A = AluOpType
    AF = ActivationFunctionType
    Q = {"V": g.vector, "A": g.scalar, "P": g.tensor, "G": g, "S": g.sync}
    count = {}
    known = {q: {} for q in Q}
    clocks = {}
    writer, readers = {}, {}

    def wait(q, tok):
        sem, n = tok
        k = known[q]
        if k.get(sem, 0) >= n:
            return
        Q[q].wait_ge(T.sem[sem], n)
        k[sem] = n
        for s2, n2 in clocks.get(tok, {}).items():
            if k.get(s2, 0) < n2:
                k[s2] = n2

    def op(q, fn, r=(), w=(), sem=None, inc=1, x=()):
        deps = []
        for key in tuple(r) + tuple(x):
            if key in writer:
                deps.append(writer[key])
        for key in x:
            deps.extend(t for t in readers.get(key, ()) if t[0] != "c" + q)
        for key in w:
            if key in writer and not (q == "P" and writer[key][0] == "cP"):
                deps.append(writer[key])
            deps.extend(readers.get(key, ()))
        deps.sort(key=lambda t: -t[1])
        for t in deps:
            wait(q, t)
        sem = sem or "c" + q
        count[sem] = count.get(sem, 0) + inc
        tok = (sem, count[sem])
        fn().then_inc(T.sem[sem], inc)
        clocks[tok] = dict(known[q])
        for key in w:
            writer[key] = tok
            readers[key] = []
        for key in tuple(r) + tuple(x):
            readers.setdefault(key, []).append(tok)
        return tok

    def arrives(key, sem, n):
        count[sem] = n
        writer[key] = (sem, n)
        readers[key] = []

    V, S_, P = g.vector, g.scalar, g.tensor

    def lst(name, k):
        c0 = LISTS[name] + 8 * k
        return T.lu[:, c0:c0 + 8 - 4 * k]

    def keys(name, a, b):
        return ["%s_%d" % (name, k) for k, (lo, hi) in enumerate(CH) if lo < b and a < hi]

    def quant(qb, sb, tb, a, b, r, w, at=None):
        at = 4 * a if at is None else at
        return op("V", lambda: V.quantize_mx(qb[:, a:b], sb[:, a:b], tb[:, at:at + 4 * (b - a)]), r=r, w=w)

    def mm(bank, lq, ls, c, rq, rs, a, b, start, stop, r):
        bk = "pb%d" % bank
        return op("P", lambda: P.matmul_mx(T[bk][:, 0:b - a], lq[:, c:c + 128], ls[:, c:c + 128],
                                           rq[:, a:b], rs[:, a:b], start, stop), r=r, w=[bk])

    def ms(out, val, w):
        return op("V", lambda: V.memset(out, val), w=w)

    def ts(out, in0, s1, s2, o0, o1, r, w, x=()):
        if o1 is None:
            return op("V", lambda: V.tensor_scalar(out, in0, s1, None, o0), r=r, w=w, x=x)
        return op("V", lambda: V.tensor_scalar(out, in0, s1, s2, o0, o1), r=r, w=w, x=x)

    def tt(out, in0, in1, o, r, w, x=()):
        return op("V", lambda: V.tensor_tensor(out, in0, in1, o), r=r, w=w, x=x)

    def scan(out, d0, d1, o0, o1, r, w):
        return op("V", lambda: V.tensor_tensor_scan(out, d0, d1, 0.0, o0, o1), r=r, w=w)

    def turn(out, in_, r, w):
        return op("V", lambda: V.transpose(out, in_), r=r, w=w)

    def act(out, in_, f, r, w, x=(), **kw):
        return op("A", lambda: S_.activation(out, in_, f, **kw), r=r, w=w, x=x)

    def cp(out, in_, r, w, x=(), q="V"):
        if q == "A":
            return act(out, in_, AF.Copy, r, w, x)
        return op("V", lambda: V.tensor_copy(out, in_), r=r, w=w, x=x)

    def iota(out, pat, base, cm, w, small=False):
        if small:
            return op("G", lambda: g.iota(out, pat, base, cm, allow_small_or_imprecise_dtypes=True), w=w)
        return op("G", lambda: g.iota(out, pat, base, cm), w=w)

    def dma(q, out, in_, sem, r=(), w=()):
        return op(q, lambda: Q[q].dma_start(out, in_), r=r, w=w, sem=sem, inc=16)

    NENG = min(len(topo.engines(a, b)) for a in T.cores for b in T.cores if a != b)

    def send(dst, out, in_, rsem, r):
        for key in r:
            wait("G", writer[key])
        rid, pid, _e = topo.addr(dst)
        eng = topo.engines(core, dst)[:NENG]
        g.remote_dma(out, in_, T.sem[rsem], T.sem.left, pid, rid, sum(1 << e for e in eng))
        count["left"] = count.get("left", 0) + len(eng)

    def weave(*chains):
        for i in range(max(len(c) for c in chains)):
            for c in chains:
                if i < len(c) and c[i] is not None:
                    c[i]()

    dma("A", T.ut[:], T.u[:], "d0", w=["ut"])
    for k, (lo, hi) in enumerate(CH):
        dma("S", T.xt[:, 4 * lo:4 * hi], T.x[:, 4 * lo:4 * hi], "d%d" % (1 + k), w=["xt_%d" % k])
    for G in range(8):
        s = 20 * (G & 1) + 2 * (G >> 1)
        dma("S", T.cdl[16 * G:16 * G + 16, 0:454], T.cd[:, s:s + 454], "d5", w=["cdl%d" % G])
    writer["cdl"] = ("d5", count["d5"])
    dma("S", T.wq[:].bitcast(dt.uint8), T.wc[:], "d6", w=["wq"])
    dma("S", T.wsc[:], T.ws[:], "d6", w=["wsc"])
    writer["wq"] = writer["wsc"]
    dma("S", T.vt[:], T.v[:], "d7", w=["vt"])

    def bf(i):
        return T.bf[:, i:i + 1]

    def cf(i):
        return T.cf[:, i:i + 1]

    def fo(i):
        return T.fo[:, 32 * i:32 * i + 1]

    ms(T.warm[:], 0.0, ["warm"])
    ms(T.ft5[:], 0.0, ["z5"])
    iota(T.ip[:], [[0, 2]], 0, 1, ["ip"])
    iota(T.li[:, 0:8], [[16, 8]], 0, 0, ["li_u"])
    iota(T.i16[:], [[0, CUT // 16], [1, 16]], 0, 0, ["i16"], True)
    op("G", lambda: g.affine_select(T.et[:], T.ft5[:, 0:1032], [[-1, 2], [1, 516]], A.not_equal, 1.0, -2, -4), r=["z5"], w=["et"])
    iota(T.dgi[:, 0:256], [[1, 8], [0, 32]], 0, 0, ["dgi0"], True)
    iota(T.dgi[:, 256:512], [[0, 8], [1, 8], [0, 4]], 0, 0, ["dgi1"], True)
    iota(T.cmi[:], [[0, 8], [1, 8], [0, 8]], 0, 0, ["cmi"], True)
    iota(T.tb[:], [[0, 3], [-1, 8], [1, 8]], 0, 0, ["tb"], True)
    iota(T.ic[:], [[1, C]], 0, 0, ["ic"], True)
    iota(T.fi[:, 0:16], [[0, 8], [8, 2]], 0, 0, ["fi0"], True)
    iota(T.fi[:, 16:32], [[0, 8], [-4, 2]], 8, 0, ["fi7"], True)
    for i, pat in enumerate(([[0, 8], [1, 2], [0, 2]], [[0, 4], [1, 2], [0, 4]], [[0, 2], [4, 2], [0, 8]],
                             [[0, 4], [1, 8]], [[0, 4], [8, 8]], [[0, 2], [2, 2], [0, 8]])):
        iota(T.fi[:, 32 * i + 32:32 * i + 64], pat, 0, 0, ["fi%d" % (i + 1)], True)
    iota(T.li[:, 8:20], [[-8, 3], [0, 4]], 16, 0, ["li_w0", "li_w1"])
    for name, pats in (("v", (([[0, 2], [64, 2], [0, 2]], 7), ([[0, 4]], 7))),
                       ("uu", (([[1, 2], [-8, 2], [4, 2]], 40), ([[1, 2], [4, 2]], 24))),
                       ("pc", (([[1, 2], [64, 2], [4, 2]], 0), ([[1, 2], [4, 2]], 0)))):
        for k, (pat, base) in enumerate(pats):
            c0 = LISTS[name] + 8 * k
            iota(T.li[:, c0:c0 + 8 - 4 * k], pat, base, 0, ["li_%s%d" % (name, k)])

    act(T.warm[:, 1:2], T.warm[:, 0:1], AF.Exp, ["warm"], ["warm1"])
    ts(T.bi[:, 0:1], T.ip[:, 0:1], 15, None, A.bitwise_and, None, ["ip"], ["bi0"])
    ts(T.bi[:, 1:2], T.ip[:, 0:1], 4, None, A.arith_shift_right, None, ["ip"], ["bi1"])
    ts(T.bi[:, 2:3], T.ip[:, 0:1], 5, 1, A.arith_shift_right, A.bitwise_and, ["ip"], ["bi2"])
    ts(T.bi[:, 3:4], T.ip[:, 0:1], 6, None, A.arith_shift_right, None, ["ip"], ["bi3"])
    cp(T.lu[:, 0:8], T.li[:, 0:8], ["li_u"], ["lu_u"])
    ms(T.keep[:], 1.0, ["keep"])
    ms(T.rmin[:], -2.0 ** 30, ["rmin"])
    cp(T.bf[:], T.bi[:], ["bi%d" % i for i in range(4)], ["bf"])
    ms(T.dtl[:, 0:512], 0.0, ["dtl0"])
    ts(cf(0), bf(0), -2.0 ** 90, None, A.mult, None, ["bf"], ["cf0"])
    ms(T.dtl[:, 768:1024], 0.0, ["dtl2"])
    ms(T.keep[:, 0:192:8], 0.0, ["keep"])
    ms(T.rmin[:, 0:128:8], 2.0 ** 30, ["rmin"])
    act(T.rst[:], T.i16[:], AF.Identity, ["i16"], ["rst"], scale=2.0 ** 96, bias=-2.0 ** 95)
    act(T.negm[:], T.i16[:], AF.Abs, ["i16", "cf0"], ["negm"], scale=2.0 ** 90, bias=cf(0))
    quant(T.uq, T.us, T.ut, 0, 128, ["ut"], ["uq"])
    cp(T.urq[:].bitcast(dt.uint32), T.uq[:].bitcast(dt.uint32).indirect(T.lu[:, 0:8]), ["uq", "lu_u"], ["urq"])
    cp(T.urs[:], T.us[:].indirect(T.lu[:, 0:8]), ["uq", "lu_u"], ["urs"], q="A")

    count_tiles = [
        lambda: (ts(T.dgi[:], T.dgi[:], bf(1), 8.0, A.is_equal, A.mult, ["dgi0", "dgi1", "bf"], ["dgi0", "dgi1"]),
                 ts(T.ct[:], T.cmi[:], bf(1), 2.0 ** -10, A.is_equal, A.mult, ["cmi", "bf"], ["ct"])),
        lambda: (tt(T.dtl[:, 512:768], T.dgi[:, 0:256], T.dgi[:, 256:512], A.subtract, ["dgi0"], ["dtl1"]),
                 ts(T.ct[:, 0:512:4], T.ct[:, 0:512:4], 2.0, None, A.mult, None, ["ct"], ["ct"])),
        lambda: ts(T.dtl[:, 512:768:4], T.dtl[:, 512:768:4], 2.0, None, A.mult, None, ["dtl1"], ["dtl1"]),
        lambda: (quant(T.cq, T.cs, T.ct, 0, 128, ["ct"], ["cq"]),
                 quant(T.dq, T.ds, T.dtl, 0, 256, ["dtl0", "dtl1", "dtl2"], ["dq"])),
    ]

    def unpack_tiles():
        for b in range(4):
            quant(T.eq, T.es, T.et, 128 * b, 128 * b + 128, ["et"], ["eq%d" % b], at=516 * (b % 2) + 2 - b // 2 * 2)

    def column_terms():
        n1 = len(ALATE)
        n0 = len(AEARLY) + sum(1 for m in ALATE if m not in AEARLY + VEARLY)
        for k, (lo, hi) in enumerate(CH):
            act(T.ij[:, lo:hi], T.ic[:, lo:hi], AF.Identity, ["ic"], ["ij%d" % k], scale=2.0 ** -18,
                bias=(8 * (n0, n1)[k] - 1) * 2.0 ** -9)

    def candidates():
        for s in range(3):
            for h in range(2):
                c = SLOT[s] // 16 + h
                cp(T.cdu[:, 24 * s + h:24 * s + 24:2], T.cdl[:, c:c + 441:40], ["cdl"], ["cdu%d" % (2 * s + h)])

    def lists():
        for name, c1, c2 in (("w", fo(4), None), ("v", fo(5), None), ("uu", fo(6), None), ("pc", fo(5), fo(6))):
            c0 = LISTS[name]
            ts(T.lu[:, c0:c0 + 12], T.li[:, c0:c0 + 12], c1, c2, A.add, None if c2 is None else A.add,
               ["li_%s0" % name, "li_%s1" % name, "fo"], ["lu_" + name])

    final_lists = [
        lambda: turn(T.fo[:], T.fi[:], ["fi%d" % i for i in range(8)], ["fo"]),
        lambda: (ts(cf(1), fo(1), bf(2), 24.0, A.not_equal, A.mult, ["fo", "bf"], ["cf1"]),
                 ts(cf(2), fo(2), bf(3), 12.0, A.not_equal, A.mult, ["fo", "bf"], ["cf2"]),
                 ts(cf(3), bf(3), 2.0, bf(2), A.mult, A.add, ["bf"], ["cf3"]), lists()),
        lambda: (ts(cf(4), cf(1), cf(2), fo(0), A.add, A.add, ["cf1", "cf2", "fo"], ["cf4"]),
                 ts(cf(5), cf(3), fo(3), None, A.add, None, ["cf3", "fo"], ["cf5"])),
        lambda: (ts(T.lu[:, 56:57], cf(4), 2.0, cf(5), A.mult, A.add, ["cf4", "cf5"], ["lu_f0"]),
                 ts(T.lu[:, 58:59], cf(4), cf(3), None, A.add, None, ["cf4", "cf3"], ["lu_f1"])),
    ]

    cdu_keys = ["cdu%d" % i for i in range(6)]
    eq_keys = ["eq%d" % i for i in range(4)]
    LN2 = math.log(2.0)
    WHOLE = 1.5 * 2.0 ** 23

    def own_part(k, t):
        lo, hi = CH[k]
        for i in range(4 if t else 0):
            if XN[k][i] == "A":
                mm(UB[i], T.eq, T.es, 128 * i, T["tq%d" % (t - 1)], T["ts%d" % (t - 1)], lo, hi, True, False,
                   eq_keys + ["tq%d_%d" % (t - 1, k)])

    def summed(k, t):
        if t == 0:
            return
        lo, hi = CH[k]
        lq, ls = T["lq%d" % (t - 1)], T["ls%d" % (t - 1)]
        arrives("lq_%d" % k, "ha%d" % (2 * (t - 1) + k), 2 * NENG)
        for i in range(4):
            mm(UB[i], T.eq, T.es, 128 * i, lq, ls, lo, hi, XN[k][i] == "V", True, eq_keys + ["lq_%d" % k])

    def taken(k, t):
        lo, hi = CH[k]
        for i in range(4 if t else 0):
            bk = "pb%d" % UB[i]
            out, w = T.xn[:, 4 * lo + i:4 * hi:4], ["xn%d_%d" % (i, k)]
            if XN[k][i] == "V":
                tt(out, T[bk][:, 0:hi - lo], T.dtw[:, C * i + lo:C * i + hi], A.add, ["dtw%d" % i], w, x=[bk])
            else:
                cp(out, T[bk][:, 0:hi - lo], [], w, x=[bk], q="A")

    def packed(k, t):
        lo, hi = CH[k]
        src, r = (T.xn, ["xn%d_%d" % (i, k) for i in range(4)]) if t else (T.xt, ["xt_%d" % k])
        quant(T["tq%d" % t], T["ts%d" % t], src, lo, hi, r, ["tq%d_%d" % (t, k)])

    def scores(t, k, bank):
        hi = CH[k][1]
        mm(bank, T.urq, T.urs, 0, T["tq%d" % t], T["ts%d" % t], 0, hi, True, True, ["urq", "urs"] + keys("tq%d" % t, 0, hi))

    def parts(m, k):
        a, c, hi = (CUT if k and m in VEARLY + AEARLY else 0), 16 * m + 16, CH[k][1]
        return [(s, x, y) for s, x, y in (("l", a, min(c, hi)), ("r", max(a, c), hi)) if x < y]

    def thk(m):
        return keys("th", 16 * m, 16 * m + 16)

    def vrow(m, k):
        f, e = divmod(m, 4)
        k2, o = (None, None) if e == 0 else (2.0, A.mult)
        bk = "pb%d" % VB[k]
        for s, a, b in parts(m, k):
            ts(T["ft%d" % f][:, 4 * a + e:4 * b:4], T[bk][:, a:b], T.th[:, 16 * m + 15:16 * m + 16], k2,
               A.is_lt if s == "l" else A.is_le, o, thk(m), keys("f%d%d%s" % (f, e, s), a, b), x=[bk])

    def arows(rows):
        def one(i):
            m, k = rows[i]
            a, hi, j, bk = parts(m, k)[0][1], CH[k][1], i % 4, "pb%d" % AB[k]
            act(T.sg[:, C * j + a:C * j + hi], T[bk][:, a:hi], AF.Sign, thk(m), ["sg%d" % j], x=[bk],
                bias=T.th[:, 16 * m + 15:16 * m + 16], scale=-1.0)

        def two(i):
            m, k = rows[i]
            f, e = divmod(m, 4)
            for s, a, b in parts(m, k):
                act(T["ft%d" % f][:, 4 * a + e:4 * b:4], T.sg[:, C * (i % 4) + a:C * (i % 4) + b], AF.Sign, ["sg%d" % (i % 4)],
                    keys("f%d%d%s" % (f, e, s), a, b), bias=-0.5 if s == "l" else 0.5)
        for i in range(len(rows) + 2):
            if i < len(rows):
                one(i)
            if i >= 2:
                two(i - 2)

    def own_scores(k):
        lo, hi = CH[k]
        bk = "pb%d" % VB[k]
        tt(T.pm[:, lo:hi], T[bk][:, lo:hi], T.negm[:, 0:hi - lo], A.subtract, ["negm"], ["pm%d" % k], x=[bk])

    def held(k):
        lo, hi = CH[k]
        scan(T.th[:, lo:hi], T.rst[:, 0:hi - lo], T.pm[:, lo:hi], A.min, A.max, ["rst", "pm%d" % k], ["th_%d" % k])

    def ties(k):
        lo, hi = CH[k]
        bk = "pb%d" % VB[k]
        tt(T.ft5[:, 4 * lo:4 * hi:4], T[bk][:, lo:hi], T.th[:, lo:hi], A.is_equal, ["th_%d" % k, "et"], ["f50l_%d" % k], x=[bk])

    def places(t):
        done = []

        def finish(f):
            fq, fs, key = T["fq%d" % f], T["fs%d" % f], ["fq%d" % f]
            quant(fq, fs, T["ft%d" % f], 0, C,
                  ["z5"] + [x for e in range(4) for s in "lr" for x in keys("f%d%d%s" % (f, e, s), 0, C)], key)
            done.append(f)
            for s in range(3):
                mm(DB, fq, fs, SLOT[s], T.dq, T.ds, 64 * s, 192 + 64 * (s // 2), len(done) == 1 and s == 0,
                   len(done) == 6 and s == 2, ["dq"] + key)
            for x in {5: [], 6: done[4:]}.get(len(done), [f]):
                mm(CNT, T.cq, T.cs, 0, T["fq%d" % x], T["fs%d" % x], 0, C, len(done) == 1, x == done[-1] and len(done) == 6,
                   ["cq", "fq%d" % x])

        fill = list(count_tiles) if t == 0 else []

        def filler():
            if fill:
                fill.pop(0)()
        own_part(0, t)
        summed(0, t)
        taken(0, t)
        own_part(1, t)
        if not LATE1:
            summed(1, t)
        packed(0, t)
        scores(t, 0, VB[0])
        scores(t, 0, AB[0])
        if not LATE1:
            taken(1, t)
            if t:
                packed(1, t)
        own_scores(0)
        if not LATE1 and not t:
            packed(1, t)
        if LATE1:
            summed(1, t)
            taken(1, t)
        held(0)
        if LATE1:
            packed(1, t)
            ties(0)
        scores(t, 1, VB[1])
        scores(t, 1, AB[1])
        if not LATE1:
            ties(0)
        early = [(m, 0) for m in AEARLY]
        first = [(m, 1) for m in ALATE if 16 * m < CUT]
        arows(early + first[:-2])
        for m in VEARLY[:1]:
            vrow(m, 0)
        own_scores(1)
        for m in VEARLY[1:2]:
            vrow(m, 0)
        held(1)
        arows(first[-2:] + [(m, 1) for m in ALATE if 16 * m >= CUT])
        for m in VEARLY[2:]:
            vrow(m, 0)
        ties(1)

        def width(m, k):
            return CH[k][1] - parts(m, k)[0][1]
        last = {f: max([i for i, m in enumerate(ALATE) if m // 4 == f] + [-1]) for f in range(6)}
        ends = {f: 2 * sum(width(m, 1) for m in ALATE[:last[f] + 1]) for f in range(6)}
        order = sorted(range(5), key=lambda f: (last[f], -f))
        rows = [m for f in order for m in range(4 * f, 4 * f + 4) if m not in ALATE]
        due, passed = [5] + order, 0
        for i, m in enumerate(rows):
            vrow(m, 1)
            filler()
            passed += width(m, 1)
            for f in [f for f in due if not fill and ends[f] + LAG <= passed and not any(x // 4 == f for x in rows[i:])]:
                finish(f)
                due.remove(f)
                passed += C
        for f in due:
            finish(f)

    for t in range(R):
        donor = T.cores[(rank + 1 + t) % N]
        child = T.cores[(rank - 1 - t) % N]
        tq, tsc, tk = T["tq%d" % t], T["ts%d" % t], keys("tq%d" % t, 0, C)
        places(t)
        if t == 0:
            column_terms()
            unpack_tiles()
        for b in range(4):
            mm(UB[b], T.eq, T.es, 128 * b, tq, tsc, 0, C, True, True, eq_keys + tk)

        def window(b):
            bk = "pb%d" % UB[b]
            act(T.dtw[:, C * b:C * b + C], T[bk][:, 0:C], AF.Copy, [], ["dtw%d" % b], x=[bk])

        wo, wl = T["wo%d" % t], T["wl%d" % t]
        if t == 0:
            candidates()
        tt(T.fl[:], T["pb%d" % DB][:, 0:192], T.tb[:], A.is_gt, ["tb"], ["fl"], x=["pb%d" % DB])
        tt(T.pcw[:], T["pb%d" % CNT][:, 0:C], T.ij[:], A.add, ["ij0", "ij1"], ["pcw"], x=["pb%d" % CNT])
        scan(T.ps[:], T.keep[:], T.fl[:], A.mult, A.add, ["keep", "fl"], ["ps"])

        def gather(s, q):
            cp(T.gc1[:, 128 * s:128 * s + 128], T.pcw[:].indirect(T.cdu[:, 24 * s + 8 * t:24 * s + 8 * t + 8]),
               ["pcw"] + cdu_keys, ["gc%d" % s], q=q)
        gather(0, "V")
        act(wo[:, 0:24], T.ps[:, 7:192:8], AF.Exp, ["ps"], ["wo0"], scale=-LN2, bias=7 * LN2)
        cp(wo[:, 24:48], T.ps[:, 7:192:8], ["ps"], ["wo1"], q="A")
        send(donor, wl[:], wo[:], "wa%d" % t, ["wo0", "wo1"])
        gather(1, "A")
        gather(2, "A")
        for s in range(3):
            turn(T.tg[:, 128 * s:128 * s + 128], T.gc1[:, 128 * s:128 * s + 128], ["gc%d" % s], ["tg%d" % s])
        if t == 0:
            weave(final_lists)
            quant(T.vq, T.vs, T.vt, 0, 128, ["vt"], ["vq"])
        zq, zs, hq, hs, lq, ls = (T["%s%d" % (n, t)] for n in ("zq", "zs", "hq", "hs", "lq", "ls"))
        arrives("wl", "wa%d" % t, NENG)

        def chain(k):
            lo, hi = CH[k]
            a, n = 128 * k, 128 - 64 * k
            e, m0, st = 24 - 12 * k, 192 * k, 2 - k
            tgk, tgv = ["tg0", "tg1"] if k == 0 else ["tg2"], T.tg[:, 2 * a:2 * (a + n):2]
            yy, zz, ky = (T.yy[:, 192 * i + a:192 * i + a + n] for i in range(3))
            ci, cj, banks = 48 * k, 96 * k, (UB if k else (SV, SA, DB, CNT))
            ends = T.mn[:, m0 + 7:m0 + n + n // 2:8]

            def s(name):
                return "%s.%d" % (name, k)

            def whole():
                r = [s("mn"), s("mx")]
                ts(T.ci[:, ci:ci + e], ends, 2.0 ** 18, None, A.mult, None, r, [s("ci")])
                for h in range(2):
                    ts(T.ci[64 * h:64 * h + 64, ci + e:ci + 2 * e], T.mn[64 - 64 * h:128 - 64 * h, m0 + 7:m0 + n + n // 2:8],
                       2.0 ** 18, None, A.mult, None, r, [s("ci%d" % h)])

            def columns():
                r = [s("ci"), s("ci0"), s("ci1")]
                ts(T.cj[:, cj:cj + 2 * e], T.ci[:, ci:ci + 2 * e], 511, None, A.bitwise_and, None, r, [s("cj")])
                for b in range(4):
                    ts(T.cj[32 * b:32 * b + 32, cj + 2 * e:cj + 4 * e], T.ci[32 * (b ^ 1):32 * (b ^ 1) + 32, ci:ci + 2 * e], 511, None,
                       A.bitwise_and, None, r, [s("cj%d" % b)])

            def mosaic():
                for b in range(4):
                    cp(T.zt[:, 4 * lo + b:4 * hi:4], T.dtw[:, C * b:C * b + C].indirect(T.eo[:, 16 * k:16 * k + (hi - lo) // 16]),
                       ["dtw%d" % b, s("eo")], [s("zt%d" % b)], q=ZQ[k][b])

            def layer():
                quant(zq, zs, T.zt, lo, hi, [s("zt%d" % b) for b in range(4)], [s("zq")])
                for b in range(4):
                    mm(banks[b], T.wq, T.wsc, 128 * b, zq, zs, lo, hi, True, True, ["wq", s("zq")])

            def relu():
                for b in range(4):
                    bk, out = "pb%d" % banks[b], T.ht[:, 4 * lo + b:4 * hi:4]
                    if HQ[k][b] == "V":
                        ts(out, T[bk][:, 0:hi - lo], 0.0, 0.015625, A.max, A.mult, [], [s("ht%d" % b)], x=[bk])
                    else:
                        act(out, T[bk][:, 0:hi - lo], AF.Relu, [], [s("ht%d" % b)], x=[bk], scale=0.015625)

            def ship():
                quant(hq, hs, T.ht, lo, hi, [s("ht%d" % b) for b in range(4)], [s("hq")])
                send(child, lq[:, lo:hi].bitcast(dt.uint8), hq[:, lo:hi].bitcast(dt.uint8), "ha%d" % (2 * t + k), [s("hq")])
                send(child, ls[:, lo:hi], hs[:, lo:hi], "ha%d" % (2 * t + k), [s("hq")])

            return [
                lambda: ts(T.bad[:, a:a + n], tgv, TH * 2.0 ** -9, None, A.is_ge, None, tgk, [s("bad")]),
                lambda: (act(T.ub[:, a:a + n], wl[:].indirect(lst("uu", k)), AF.Exp, ["wl", "lu_uu"], [s("ub")], scale=LN2,
                             bias=-8 * LN2 + math.log(1.0 + 2.0 ** -9)),
                         tt(T.dd[:, a:a + n], wl[:].indirect(lst("w", k)), T.bad[:, a:a + n], A.mult, ["wl", "lu_w", s("bad")], [s("dd")])),
                lambda: (scan(T.vv[:, a:a + n], T.keep[:, 0:n], T.dd[:, a:a + n], A.mult, A.add, ["keep", s("dd")], [s("vv")]),
                         tt(T.pc2[:, a:a + n], tgv, T.bad[:, a:a + n], A.subtract, tgk + [s("bad")], [s("pc2")]),
                         window(2 * k), window(2 * k + 1)),
                lambda: tt(yy, T.vv[:, a:a + n].indirect(lst("v", k)), T.ub[:, a:a + n], A.mult, [s("vv"), "lu_v", s("ub")], [s("yy")]),
                lambda: ts(zz, yy, WHOLE, -(WHOLE + 64.0), A.add, A.add, [s("yy")], [s("zz")]),
                lambda: tt(ky, T.pc2[:, a:a + n].indirect(lst("pc", k)), zz, A.add, [s("zz"), s("pc2"), "lu_pc"], [s("ky")]),
                lambda: scan(T.mn[:, m0:m0 + n], T.rmin[:, 0:n], ky, A.max, A.min, ["rmin", s("ky")], [s("mn")]),
                lambda: turn(T.rb[:, 64 * k:64 * k + 64], T.mn[:, m0 + st - 1:m0 + n:st], [s("mn")], [s("rb")]),
                lambda: turn(T.mn[:, m0 + n + st - 1:m0 + n + n // 2:st], T.rb[:, 64 * k + 16:64 * k + 48], [s("rb")], [s("mx")]),
                whole, columns,
                lambda: cp(T.eo[:, 16 * k:16 * k + 16], T.cj[:, cj:cj + 4 * e].indirect(T.lu[:, 56 + 2 * k:57 + 2 * k]),
                           ["lu_f%d" % k, s("cj")] + [s("cj%d" % b) for b in range(4)], [s("eo")]),
                mosaic, layer, relu, ship]

        weave(chain(0), [None] * SKEW + chain(1))
        if t == R - 1:
            for k, (lo, hi) in enumerate(CH):
                cp(T.elb[:, lo:hi], T.ic[:].indirect(T.eo[:, 16 * k:16 * k + (hi - lo) // 16]), ["ic", "eo.%d" % k], ["elb%d" % k], q="A")
            dma("S", T.el[:], T.elb[0:128:16, :], "d8", r=["elb0", "elb1"])

    nq, ns = T["tq%d" % R], T["ts%d" % R]

    def last(k):
        lo, hi = CH[k]
        bk, key = "pb%d" % (SV + k), ["tq%d_%d" % (R, k)]

        def store():
            packed(k, R)
            mm(SV + k, T.vq, T.vs, 0, nq, ns, lo, hi, True, True, ["vq"] + key)
            dma("S", T.oc[:, 4 * lo:4 * hi], nq[:, lo:hi].bitcast(dt.uint8), "d%d" % (9 + k), r=key)
            if k:
                for i in range(4):
                    dma("AS"[i % 2], T.osc[4 * i:4 * i + 4, :], ns[32 * i:32 * i + 4, :], "d13", r=keys("tq%d" % R, 0, C))
        return [lambda: (own_part(k, R), summed(k, R), taken(k, R)), store,
                lambda: (cp(T.yb[:, lo:hi], T[bk][:, 0:hi - lo], [], ["yb%d" % k], x=[bk]),
                         dma("SA"[k], T.y[:, lo:hi], T.yb[:, lo:hi], "d%d" % (14 + k), r=["yb%d" % k]))]
    weave(last(0), [None] + last(1))

    for sem in sorted(count):
        wait("G", (sem, count[sem]))


SKEW = 0
ZQ = ("VAVA", "VAVA")
HQ = ("VAVA", "VAVA")
